import numpy as np
import ml_dtypes


def mxq(x, axis, fmt="e4m3"):
    dtype, down = {"e4m3": (ml_dtypes.float8_e4m3fn, 7), "e5m2": (ml_dtypes.float8_e5m2, 14)}[fmt]
    v = np.moveaxis(np.asarray(x, np.float32).astype(ml_dtypes.bfloat16).astype(np.float64), axis, -1)
    blocks = v.reshape(v.shape[:-1] + (-1, 32))
    amax = np.abs(blocks).max(-1, keepdims=True)
    byte = np.maximum(np.where(amax > 0, np.frexp(amax)[1] - 1 + 127, 0) - down, 1)
    scale = np.exp2(byte - 127.0)
    codes = (blocks / scale).astype(np.float32).astype(dtype).astype(np.float64)
    return np.moveaxis((codes * scale).reshape(v.shape), -1, axis)


WIDE = False


def mx_kscale(k):
    if not WIDE:
        return np.ones(k)
    levels = np.array([10, -10, 5, -5, 0])
    if k % 512:
        return np.exp2(np.random.permutation(np.resize(levels, k // 32))).repeat(32)
    a = np.empty((k // 512, 16))
    for p in range(k // 512):
        a[p, :8] = np.random.permutation(np.resize(levels, 8))
        for g in range(8):
            far = levels[np.abs(levels - a[p, g]) >= 10]
            a[p, g + 8] = far[np.random.randint(len(far))]
    return np.exp2(a.ravel()).repeat(32)


BF16 = ml_dtypes.bfloat16


def bf(x):
    return np.asarray(x, np.float32).astype(BF16)


def f64(x):
    return np.asarray(x).astype(np.float64)

def planes(Y):
    n, m = Y.shape
    b = f64(bf(Y)).reshape(n // 32, 32, m)
    amax = np.abs(b).max(1)
    byte = np.clip(np.where(amax > 0, np.frexp(amax)[1] - 1 + 127 - 7, 1), 1, 254)
    codes = (b * np.exp2(127.0 - byte)[:, None, :]).reshape(n, m).astype(np.float32).astype(ml_dtypes.float8_e4m3fn).view(np.uint8)
    words = codes.reshape(n // 512, 128, 4, m).transpose(0, 1, 3, 2)
    return np.ascontiguousarray(words), np.ascontiguousarray(byte.astype(np.uint8).reshape(n // 512, 16, m))


B, M, P, N, C, T = 512, 1024, 1024, 4096, 2, 3


def setup_inputs():
    s1, s2 = mx_kscale(M), mx_kscale(M)
    t = mx_kscale(P)
    u1 = np.random.standard_normal((B, M))
    u2 = np.random.standard_normal((B, M))
    w1 = np.random.standard_normal((M, P)) / np.sqrt(M)
    w2 = np.random.standard_normal((M, P)) / np.sqrt(M)
    coords = np.random.uniform(-1.0, 1.0, (N, C))
    wt = np.random.standard_normal((T, P)) * 1.5
    gain = 1.0 + 0.1 * np.random.standard_normal(P)
    return {
        "u1": bf(u1 * s1),
        "u2": bf(u2 * s2),
        "w1": bf(w1 / s1[:, None]),
        "w2": bf(w2 / s2[:, None] * t),
        "coords": bf(coords),
        "wt": bf(wt),
        "gain": bf(gain / t),
    }


def branch_coefficients(u1, u2, w1, w2):
    b1 = np.tanh(mxq(u1, 1, "e4m3") @ mxq(w1, 0, "e4m3"))
    b2 = mxq(u2, 1, "e4m3") @ mxq(w2, 0, "e4m3")
    return b1 * b2


def trunk_features(coords, wt, gain):
    y0 = coords[:, 0:1]
    y1 = coords[:, 1:2]
    pre = y0 * wt[0][None, :] + y1 * wt[1][None, :] + wt[2][None, :]
    return gain[None, :] * np.tanh(pre)


def core(u1, u2, w1, w2, coords, wt, gain):
    coef = branch_coefficients(f64(u1), f64(u2), f64(w1), f64(w2))
    trunk = trunk_features(f64(coords), f64(wt), f64(gain))
    p_scale = np.sqrt(coef.shape[1])
    return (mxq(coef, 1, "e4m3") @ mxq(trunk, 1, "e4m3").T) / p_scale


def reference(u1, u2, w1, w2, coords, wt, gain):
    R_out = core(u1, u2, w1, w2, coords, wt, gain)
    words, scales = planes(R_out.T)
    return R_out, words, scales

@@ -1,0 +1,442 @@
+from contextlib import ExitStack
+
+import concourse.mybir as mybir
+from concourse.masks import make_identity
+
+B, M, P, N = 512, 1024, 1024, 4096
+FLOPS = 2 * (2 * B * M * P) + 2 * B * N * P
+
+F32 = mybir.dt.float32
+BF16 = mybir.dt.bfloat16
+U32 = mybir.dt.uint32
+I32 = mybir.dt.int32
+U8 = mybir.dt.uint8
+FP8X4 = mybir.dt.float8_e4m3fn_x4
+ALU = mybir.AluOpType
+ACT = mybir.ActivationFunctionType
+
+TINY = 2.0 ** -60
+GAIN_ON_GPSIMD = 3
+LAY_S = 2000
+NARROW_S = 870
+ROWS_PER_STORE = 2
+
+
+def tile_multipleinputoperatorbranchtrunk_x1_kernel(
+    tc, u1, u2, w1, w2, coords, wt, gain, out_0, out_1, out_2
+):
+    nc = tc.nc
+    with ExitStack() as ctx:
+        keep = ctx.enter_context(tc.tile_pool(name="keep", bufs=1))
+        work = ctx.enter_context(tc.tile_pool(name="work", bufs=2))
+        ps_fix = ctx.enter_context(tc.psum_pool(name="ps_fix", bufs=1))
+        ps_x = ctx.enter_context(tc.psum_pool(name="ps_x", bufs=3))
+        ps = ctx.enter_context(tc.psum_pool(name="ps", bufs=4))
+        head = ctx.enter_context(tc.tile_pool(name="head", bufs=1))
+
+        crd = keep.tile([128, 32, 2], BF16, name="crd")
+        nc.sync.dma_start(
+            out=crd[:].rearrange("p (h t) c -> p h (t c)", t=4),
+            in_=coords.rearrange("(h p t) c -> p h (t c)", p=128, t=4),
+        )
+        prow = keep.tile([128, P], BF16, name="prow")
+        nc.vector.memset(prow[:], 0.0)
+        nc.sync.dma_start(out=prow[0:3, :], in_=wt)
+        nc.sync.dma_start(out=prow[3:4, :], in_=gain.unsqueeze(0))
+        id_bf = keep.tile([128, 128], BF16, name="id_bf")
+        make_identity(nc, id_bf[:])
+        id_f32 = keep.tile([128, 128], F32, name="id_f32")
+        make_identity(nc, id_f32[:])
+
+        uraw, wraw = {}, {}
+
+        def load_u(i, u):
+            uraw[i] = head.tile([128, 4, M], BF16, name=f"uraw{i}")
+            nc.sync.dma_start(out=uraw[i][:], in_=u.rearrange("(b p) m -> p b m", p=128))
+
+        def load_w(i, g, w):
+            wraw[i, g] = head.tile([128, 4, P], BF16, name="wr", tag="wraw", bufs=3)
+            nc.sync.dma_start(
+                out=wraw[i, g][:], in_=w[512 * g : 512 * (g + 1), :].rearrange("(p j) c -> p j c", j=4)
+            )
+
+        load_w(0, 0, w1)
+        load_u(0, u1)
+        load_w(0, 1, w1)
+        load_u(1, u2)
+        load_w(1, 0, w2)
+        load_w(1, 1, w2)
+
+        tq = keep.tile([128, 8, 2, 512], U32, name="tq", align_bytes=64)
+        ts = keep.tile([128, 8, 2, 512], U8, name="ts", align_bytes=64)
+        cq = keep.tile([128, 2, B], U32, name="cq", align_bytes=64)
+        cs = keep.tile([128, 2, B], U8, name="cs", align_bytes=64)
+        rrow = keep.tile([128, 8, 128], F32, name="rrow")
+        par = keep.tile([128, 4, 8], F32, name="par")
+        w0s = keep.tile([128, 8], F32, name="w0s")
+        rat = keep.tile([128, 8], F32, name="rat")
+        tmpa = keep.tile([128, 8], F32, name="tmpa")
+        tmpb = keep.tile([128, 8], F32, name="tmpb")
+
+        V, S = "vector", "scalar"
+
+        prm = ps_fix.tile([128, 8, 128], BF16, name="prm")
+        for s in range(8):
+            g, t = divmod(s, 4)
+            nc.tensor.transpose(prm[:, s, :], prow[:, 512 * g + t : 512 * (g + 1) : 4], id_bf[:])
+        nc.vector.tensor_copy(out=par[:].rearrange("p v s -> p s v"), in_=prm[:, :, 0:4])
+        nc.vector.tensor_single_scalar(tmpa[:], par[:, 0, :], TINY, ALU.is_lt)
+        nc.vector.scalar_tensor_tensor(
+            out=tmpb[:], in0=par[:, 0, :], scalar=-TINY, in1=tmpa[:], op0=ALU.is_gt, op1=ALU.mult
+        )
+        nc.vector.scalar_tensor_tensor(
+            out=w0s[:], in0=tmpb[:], scalar=2.0 * TINY, in1=par[:, 0, :], op0=ALU.mult, op1=ALU.add
+        )
+        nc.vector.reciprocal(tmpa[:], w0s[:])
+        nc.vector.tensor_mul(rat[:], tmpa[:], par[:, 1, :])
+        for half in range(2):
+            rb = ps.tile([128, 4, 128], F32, name="rb", tag="acc")
+            for t in range(4):
+                s = 4 * half + t
+                nc.tensor.transpose(rb[:, t, :], rat[:, s : s + 1].to_broadcast([128, 128]), id_f32[:])
+            if half:
+                nc.vector.tensor_copy(out=rrow[:, 4 * half : 4 * half + 4, :], in_=rb[:])
+            else:
+                nc.scalar.copy(out=rrow[:, 4 * half : 4 * half + 4, :], in_=rb[:])
+
+        def scaled(engine, dst, src):
+            if engine == V:
+                nc.vector.tensor_scalar(dst, src, 0.03125, None, ALU.mult)
+            else:
+                nc.scalar.mul(dst, src, 0.03125)
+
+        def moved(engine, dst, src):
+            if engine == V:
+                nc.vector.tensor_copy(out=dst, in_=src)
+            else:
+                nc.scalar.copy(out=dst, in_=src)
+
+        def quantize(codes, scales, src):
+            nc.vector.quantize_mx(out=codes.bitcast(FP8X4), scales=scales, in_=src)
+
+
+        uq, us, wq, ws = {}, {}, {}, {}
+        for i in range(2):
+            uq[i] = head.tile([128, 2, B], U32, name=f"uq{i}", align_bytes=64)
+            us[i] = head.tile([128, 2, B], U8, name=f"us{i}", align_bytes=64)
+            wq[i] = head.tile([128, 2, P], U32, name=f"wq{i}", align_bytes=64)
+            ws[i] = head.tile([128, 2, P], U8, name=f"ws{i}", align_bytes=64)
+        ugs, wgs, cfs = {}, {}, {}
+
+        def u_turn(i, g, half):
+            def job(engine):
+                if (g, half) == (0, 0):
+                    ugs[i] = head.tile([128, 2, B, 4], BF16, name="ug", align_bytes=64)
+                words_out = ugs[i][:, g, :, :].rearrange("p r t -> p (r t)").bitcast(F32)
+                ut = ps.tile([128, 2, 256], F32, name="ut", tag="acc")
+                for r in range(2):
+                    words = uraw[i][:, 2 * half + r, :].bitcast(F32)
+                    for k in range(2):
+                        nc.tensor.transpose(
+                            ut[:, k, 128 * r : 128 * (r + 1)],
+                            words[:, 256 * g + k : 256 * (g + 1) : 2],
+                            id_f32[:],
+                        )
+                dst = words_out[:, 512 * half : 512 * (half + 1)].rearrange("p (r k) -> p r k", k=2)
+                src = ut[:].rearrange("p k r -> p r k")
+                moved(engine, dst, src)
+            return job
+
+        def u_quant(i):
+            def job(engine):
+                quantize(
+                    uq[i][:].rearrange("p g b -> p (g b)"), us[i][:].rearrange("p g b -> p (g b)"),
+                    ugs[i][:].rearrange("p g r t -> p (g r t)"),
+                )
+            return job
+
+        def w_lay(i, g, half):
+            def job(engine):
+                if half == 0:
+                    wgs[i, g] = head.tile([128, 4 * P], BF16, name="wgt", tag="wg", align_bytes=64, bufs=2)
+                dst = wgs[i, g][:, 2048 * half : 2048 * (half + 1)].rearrange("p (t m j) -> p t m j", t=4, j=4)
+                src = wraw[i, g][:, :, 512 * half : 512 * (half + 1)].rearrange("p j (m t) -> p t m j", t=4)
+                moved(engine, dst, src)
+            return job
+
+        def w_quant(i, g):
+            def job(engine):
+                quantize(wq[i][:, g, :], ws[i][:, g, :], wgs[i, g][:])
+            return job
+
+        def branch(i, G, b):
+            acc = ps.tile([128, 4, 128], F32, name="br", tag="acc")
+            for t in range(4):
+                f = slice(512 * G + 128 * t, 512 * G + 128 * (t + 1))
+                r = slice(128 * b, 128 * (b + 1))
+                for g in range(2):
+                    nc.tensor.matmul_mx(
+                        out=acc[:, t, :],
+                        lhsT=wq[i][:, g, f].bitcast(FP8X4), lhsT_scale=ws[i][:, g, f],
+                        rhs=uq[i][:, g, r].bitcast(FP8X4), rhs_scale=us[i][:, g, r],
+                        start=(g == 0), stop=(g == 1),
+                    )
+            return acc
+
+        b1s = {}
+
+        def branch1(G, b):
+            def job(engine):
+                a1 = branch(0, G, b)
+                b1s[G, b] = head.tile([128, 128, 4], F32, name="b1", bufs=3)
+                nc.scalar.activation(out=b1s[G, b][:], in_=a1[:].rearrange("p t b -> p b t"), func=ACT.Tanh)
+            return job
+
+        def branch2(G, b):
+            def job(engine):
+                if b == 0:
+                    cfs[G] = head.tile([128, B, 4], BF16, name="cf", align_bytes=64)
+                a2 = branch(1, G, b)
+                nc.vector.tensor_tensor(
+                    cfs[G][:, 128 * b : 128 * (b + 1), :], a2[:].rearrange("p t b -> p b t"), b1s[G, b][:], ALU.mult
+                )
+            return job
+
+        def coef_quant(G):
+            def job(engine):
+                quantize(cq[:, G, :], cs[:, G, :], cfs[G][:].rearrange("p b t -> p (b t)"))
+            return job
+
+        tiles = {}
+
+        def rows(bt, hh):
+            def job(engine):
+                bs = slice(128 * bt, 128 * (bt + 1))
+                if bt == 0:
+                    tiles[hh] = head.tile([128, 4, 512], F32, name="o", tag="wraw", bufs=3)
+                h = hh
+                acc = ps.tile([128, 512], F32, name="oa", tag="acc")
+                for G in range(2):
+                    nc.tensor.matmul_mx(
+                        out=acc[:],
+                        lhsT=cq[:, G, bs].bitcast(FP8X4), lhsT_scale=cs[:, G, bs],
+                        rhs=tq[:, h, G, :].bitcast(FP8X4), rhs_scale=ts[:, h, G, :],
+                        start=(G == 0), stop=(G == 1),
+                    )
+                scaled(
+                    engine,
+                    tiles[hh][:, bt, :].rearrange("b (p t) -> b p t", t=4),
+                    acc[:].rearrange("b (t p) -> b p t", t=4),
+                )
+                if bt % ROWS_PER_STORE == ROWS_PER_STORE - 1:
+                    b0 = bt + 1 - ROWS_PER_STORE
+                    nc.sync.dma_start(
+                        out=out_0[128 * b0 : 128 * (bt + 1), 512 * h : 512 * (h + 1)].rearrange("(b p) n -> p b n", p=128),
+                        in_=tiles[hh][:, b0 : bt + 1, :],
+                    )
+            return job
+
+        def narrow(hh, pair):
+            def job(engine):
+                if pair == 0:
+                    tiles["n", hh] = head.tile([128, 4, 512], BF16, name="ob", tag="ob", bufs=2)
+                dst = tiles["n", hh][:, 2 * pair : 2 * pair + 2, :]
+                src = tiles[hh][:, 2 * pair : 2 * pair + 2, :]
+                moved(engine, dst, src)
+            return job
+
+        def plane(hh, pair):
+            def job(engine):
+                if pair == 0:
+                    tiles["p", hh] = head.tile([128, B, 4], BF16, name="pl", align_bytes=64, tag="wg", bufs=2)
+                ut = ps.tile([128, 2, 256], F32, name="pt", tag="acc")
+                for r in range(2):
+                    words = tiles["n", hh][:, 2 * pair + r, :].bitcast(F32)
+                    for k in range(2):
+                        nc.tensor.transpose(ut[:, k, 128 * r : 128 * (r + 1)], words[:, k:256:2], id_f32[:])
+                dst = tiles["p", hh][:].rearrange("p b t -> p (b t)").bitcast(F32)
+                dst = dst[:, 512 * pair : 512 * (pair + 1)].rearrange("p (r k) -> p r k", k=2)
+                src = ut[:].rearrange("p k r -> p r k")
+                moved(engine, dst, src)
+            return job
+
+        def plane_quant(hh):
+            def job(engine):
+                h = hh
+                pq = head.tile([128, B], U32, name="pq", align_bytes=64, bufs=3)
+                pc = head.tile([128, B], U8, name="pc", align_bytes=64, bufs=3)
+                quantize(pq[:], pc[:], tiles["p", hh][:].rearrange("p b t -> p (b t)"))
+                nc.sync.dma_start(
+                    out=out_1[h].rearrange("p m t -> p (m t)").bitcast(I32), in_=pq[:].bitcast(I32)
+                )
+                for q in range(4):
+                    nc.sync.dma_start(
+                        out=out_2[h, 4 * q : 4 * q + 4, :].bitcast(I32),
+                        in_=pc[32 * q : 32 * q + 4, :].bitcast(I32),
+                    )
+            return job
+
+        lines, ths, grps = {}, {}, {}
+        block = [0]
+
+        def line(h, t):
+            lines[h, t] = work.tile([128, 8, 128], F32, name="line", bufs=6)
+            b = 4 * h + t
+            args = (lines[h, t][:], rrow[:], crd[:, b, 1:2], crd[:, b, 0:1], ALU.mult, ALU.add)
+            nc.vector.tensor_scalar(*args)
+
+        def feature(h, s):
+            g, t = divmod(s, 4)
+            if t == 0:
+                ths[h, g] = work.tile([128, 4, 512], F32, name="th", bufs=4)
+            pres = []
+            for f in range(2):
+                pre = ps_x.tile([128, 4, 128], F32, name="pre")
+                for b in range(4):
+                    nc.tensor.transpose(pre[:, b, :], lines[h, b][:, s + f, :], id_f32[:])
+                pres.append(pre)
+            for f in range(2):
+                nc.scalar.activation(
+                    out=ths[h, g][:, t + f, :], in_=pres[f][:].rearrange("p b n -> p (b n)"), func=ACT.Tanh,
+                    scale=w0s[:, s + f : s + f + 1], bias=par[:, 2, s + f : s + f + 1],
+                )
+
+        def gain_block(h, g, b):
+            if h not in grps:
+                grps[h] = work.tile([128, 2, 512, 4], BF16, name="grp", align_bytes=64, bufs=1)
+            src = ths[h, g][:, :, 128 * b : 128 * (b + 1)].rearrange("p t n -> p n t")
+            dst = grps[h][:, g, 128 * b : 128 * (b + 1), :]
+            if 4 * g + b >= GAIN_ON_GPSIMD:
+                nc.vector.tensor_tensor(
+                    dst, src, prm[:, 4 * g : 4 * g + 4, 3].unsqueeze(1).to_broadcast([128, 128, 4]), ALU.mult
+                )
+            else:
+                nc.gpsimd.tensor_tensor(
+                    dst, src, par[:, 3, 4 * g : 4 * g + 4].unsqueeze(1).to_broadcast([128, 128, 4]), ALU.mult
+                )
+
+        def trunk_quant(h):
+            quantize(
+                tq[:, h, :, :].rearrange("p g n -> p (g n)"), ts[:, h, :, :].rearrange("p g n -> p (g n)"),
+                grps[h][:].rearrange("p g n t -> p (g n t)"),
+            )
+
+        def each(*fns):
+            for fn in fns:
+                fn()
+
+        load = {V: 0.0, S: 0.0}
+        todo = []
+        locked = []
+        credit = [0.0]
+
+        def add(job, cost_v, cost_s, only=None, then=()):
+            todo.append((job, {V: cost_v, S: cost_s}, only, then))
+
+        def run(amount):
+            credit[0] += amount
+            while todo and credit[0] > 0.0:
+                job, cost, only, then = todo[0]
+                todo.remove(todo[0])
+                engine = only
+                if engine is None:
+                    engine = V if load[V] + cost[V] <= load[S] + cost[S] else S
+                job(engine)
+                load[engine] += cost[engine]
+                credit[0] -= cost[engine]
+                locked.extend(then)
+
+        def quant(fn, cols):
+            load[V] += 12 + 0.22 * cols
+            fn(V)
+
+        def add_rows(h):
+            for bt in range(4):
+                add(rows(bt, h), 440, 445, then=((narrow_then_plane, h, bt // 2),) if bt % 2 == 1 else ())
+
+        def narrow_then_plane(h, pair):
+            engine = V if load[V] + 460 <= load[S] + NARROW_S else S
+            load[engine] += {V: 460, S: 870}[engine]
+            narrow(h, pair)(engine)
+            add(plane(h, pair), 440, 445, then=((quant, plane_quant(h), 2048),) if pair else ())
+
+        def flush():
+            now = locked[:]
+            locked.clear()
+            for fn, *args in now:
+                fn(*args)
+
+        def lay(i, g, half):
+            add(w_lay(i, g, half), 1050, LAY_S, then=((quant, w_quant(i, g), 4096),) if half else ())
+
+        def turn(i):
+            for g in range(2):
+                for half in range(2):
+                    add(u_turn(i, g, half), 440, 445, then=((quant, u_quant(i), 4096),) if (g, half) == (1, 1) else ())
+
+        order = [(G, b) for G in range(2) for b in range(4)]
+        chunks_done = []
+        coef_done = []
+
+        def coef_end():
+            quant(coef_quant(0), 2048)
+            quant(coef_quant(1), 2048)
+            coef_done.append(True)
+            for h in chunks_done:
+                add_rows(h)
+
+        for t in range(4):
+            line(0, t)
+        load[V] += 1760
+        lay(0, 0, 0)
+        lay(0, 0, 1)
+        turn(0)
+        lay(0, 1, 0)
+        lay(0, 1, 1)
+        turn(1)
+        lay(1, 0, 0)
+        lay(1, 0, 1)
+        lay(1, 1, 0)
+        lay(1, 1, 1)
+
+        def pair_job(k):
+            def job(engine):
+                flush()
+                if k < 8:
+                    branch1(*order[k])(S)
+                    load[S] += 470
+                if k >= 2:
+                    branch2(*order[k - 2])(V)
+                    load[V] += 440
+            return job
+
+        for k in range(10):
+            add(pair_job(k), 0, 0, only=V, then=((coef_end,),) if k == 9 else ())
+
+        first = (3000.0, 9000.0)
+        run(first[0])
+        for h in range(10):
+            if h < 7:
+                for t in range(4):
+                    line(h + 1, t)
+                load[V] += 1760
+            rate = (first[1] if not coef_done else 5000.0) / 4
+            for s in range(0, 8, 2):
+                if h < 8:
+                    feature(h, s)
+                    load[S] += 940
+                run(rate)
+                flush()
+            if 2 <= h < 10:
+                quant(lambda engine: trunk_quant(h - 2), 4096)
+                chunks_done.append(h - 2)
+                if coef_done:
+                    add_rows(h - 2)
+            if 1 <= h < 9:
+                for g in range(2):
+                    for b in range(4):
+                        gain_block(h - 1, g, b)
+                load[V] += 440 * (8 - GAIN_ON_GPSIMD)
+        while todo or locked:
+            run(900.0)
+            flush()

@@ -16,10 +16,20 @@ ALU = mybir.AluOpType
 ACT = mybir.ActivationFunctionType
 
 TINY = 2.0 ** -60
+V, S = "vector", "scalar"
+
 GAIN_ON_GPSIMD = 3
-LAY_S = 2000
-NARROW_S = 870
-ROWS_PER_STORE = 2
+LINES_ON_GPSIMD = 0
+LAG_GAIN = 1
+LAG_QUANT = 2
+FIRST_BUDGET = 3000.0
+HEAD_BUDGET = 9000.0
+OUT_BUDGET = 5000.0
+COST = {
+    "bank": {V: 440.0, S: 445.0},
+    "lay": {V: 530.0, S: 1000.0},
+    "narrow": {V: 440.0, S: 870.0},
+}
 
 
 def tile_multipleinputoperatorbranchtrunk_x1_kernel(
@@ -29,30 +39,14 @@ def tile_multipleinputoperatorbranchtrunk_x1_kernel(
     with ExitStack() as ctx:
         keep = ctx.enter_context(tc.tile_pool(name="keep", bufs=1))
         work = ctx.enter_context(tc.tile_pool(name="work", bufs=2))
+        head = ctx.enter_context(tc.tile_pool(name="head", bufs=1))
         ps_fix = ctx.enter_context(tc.psum_pool(name="ps_fix", bufs=1))
         ps_x = ctx.enter_context(tc.psum_pool(name="ps_x", bufs=3))
         ps = ctx.enter_context(tc.psum_pool(name="ps", bufs=4))
-        head = ctx.enter_context(tc.tile_pool(name="head", bufs=1))
 
-        crd = keep.tile([128, 32, 2], BF16, name="crd")
-        nc.sync.dma_start(
-            out=crd[:].rearrange("p (h t) c -> p h (t c)", t=4),
-            in_=coords.rearrange("(h p t) c -> p h (t c)", p=128, t=4),
-        )
-        prow = keep.tile([128, P], BF16, name="prow")
-        nc.vector.memset(prow[:], 0.0)
-        nc.sync.dma_start(out=prow[0:3, :], in_=wt)
-        nc.sync.dma_start(out=prow[3:4, :], in_=gain.unsqueeze(0))
-        id_bf = keep.tile([128, 128], BF16, name="id_bf")
-        make_identity(nc, id_bf[:])
-        id_f32 = keep.tile([128, 128], F32, name="id_f32")
-        make_identity(nc, id_f32[:])
-
-        uraw, wraw = {}, {}
-
-        def load_u(i, u):
-            uraw[i] = head.tile([128, 4, M], BF16, name=f"uraw{i}")
-            nc.sync.dma_start(out=uraw[i][:], in_=u.rearrange("(b p) m -> p b m", p=128))
+        small = keep.tile([128, P], BF16, name="small")
+        nc.vector.memset(small[:], 0.0)
+        wraw = {}
 
         def load_w(i, g, w):
             wraw[i, g] = head.tile([128, 4, P], BF16, name="wr", tag="wraw", bufs=3)
@@ -60,31 +54,56 @@ def tile_multipleinputoperatorbranchtrunk_x1_kernel(
                 out=wraw[i, g][:], in_=w[512 * g : 512 * (g + 1), :].rearrange("(p j) c -> p j c", j=4)
             )
 
+        nc.sync.dma_start(out=small[0:3, :], in_=wt)
+        nc.sync.dma_start(out=small[3:4, :], in_=gain.unsqueeze(0))
+        nc.sync.dma_start(out=small[32:64, 0:256], in_=coords.rearrange("(k p) c -> k (p c)", p=128))
         load_w(0, 0, w1)
-        load_u(0, u1)
-        load_w(0, 1, w1)
-        load_u(1, u2)
+        uraw = {}
+        for i, u in ((0, u1), (1, u2)):
+            uraw[i] = head.tile([128, 4, M], BF16, name=f"uraw{i}")
+            nc.sync.dma_start(out=uraw[i][:], in_=u.rearrange("(b p) m -> p b m", p=128))
+            if i == 0:
+                load_w(0, 1, w1)
         load_w(1, 0, w2)
         load_w(1, 1, w2)
+
+        id_bf = keep.tile([128, 128], BF16, name="id_bf")
+        make_identity(nc, id_bf[:])
+        id_f32 = keep.tile([128, 128], F32, name="id_f32")
+        make_identity(nc, id_f32[:])
 
         tq = keep.tile([128, 8, 2, 512], U32, name="tq", align_bytes=64)
         ts = keep.tile([128, 8, 2, 512], U8, name="ts", align_bytes=64)
         cq = keep.tile([128, 2, B], U32, name="cq", align_bytes=64)
         cs = keep.tile([128, 2, B], U8, name="cs", align_bytes=64)
-        rrow = keep.tile([128, 8, 128], F32, name="rrow")
+        uq, us, wq, ws = {}, {}, {}, {}
+        for i in range(2):
+            uq[i] = head.tile([128, 2, B], U32, name=f"uq{i}", align_bytes=64)
+            us[i] = head.tile([128, 2, B], U8, name=f"us{i}", align_bytes=64)
+            wq[i] = head.tile([128, 2, P], U32, name=f"wq{i}", align_bytes=64)
+            ws[i] = head.tile([128, 2, P], U8, name=f"ws{i}", align_bytes=64)
+
+        turned = keep.tile([128, P], BF16, name="turned")
+        nc.vector.tensor_copy(
+            out=turned[:].rearrange("p (t i r) -> p t i r", t=4, r=4),
+            in_=small[:].rearrange("p (i t r) -> p t i r", t=4, r=4),
+        )
+        xy = keep.tile([128, 2, 32], F32, name="xy")
+        xyp = ps.tile([128, 2, 128], BF16, name="xyp", tag="acc")
+        for c in range(2):
+            nc.tensor.transpose(xyp[:, c, :], small[:, c:256:2], id_bf[:])
+        prm = ps_fix.tile([128, 8, 128], BF16, name="prm")
+        for s in range(8):
+            G, t = divmod(s, 4)
+            col = 256 * t + 128 * G
+            nc.tensor.transpose(prm[:, s, :], turned[:, col : col + 128], id_bf[:])
         par = keep.tile([128, 4, 8], F32, name="par")
         w0s = keep.tile([128, 8], F32, name="w0s")
         rat = keep.tile([128, 8], F32, name="rat")
         tmpa = keep.tile([128, 8], F32, name="tmpa")
         tmpb = keep.tile([128, 8], F32, name="tmpb")
-
-        V, S = "vector", "scalar"
-
-        prm = ps_fix.tile([128, 8, 128], BF16, name="prm")
-        for s in range(8):
-            g, t = divmod(s, 4)
-            nc.tensor.transpose(prm[:, s, :], prow[:, 512 * g + t : 512 * (g + 1) : 4], id_bf[:])
         nc.vector.tensor_copy(out=par[:].rearrange("p v s -> p s v"), in_=prm[:, :, 0:4])
+        nc.scalar.copy(out=xy[:], in_=xyp[:, :, 32:64])
         nc.vector.tensor_single_scalar(tmpa[:], par[:, 0, :], TINY, ALU.is_lt)
         nc.vector.scalar_tensor_tensor(
             out=tmpb[:], in0=par[:, 0, :], scalar=-TINY, in1=tmpa[:], op0=ALU.is_gt, op1=ALU.mult
@@ -94,21 +113,16 @@ def tile_multipleinputoperatorbranchtrunk_x1_kernel(
         )
         nc.vector.reciprocal(tmpa[:], w0s[:])
         nc.vector.tensor_mul(rat[:], tmpa[:], par[:, 1, :])
-        for half in range(2):
+        rrow = keep.tile([128, 8, 128], F32, name="rrow")
+        for G in range(2):
             rb = ps.tile([128, 4, 128], F32, name="rb", tag="acc")
             for t in range(4):
-                s = 4 * half + t
+                s = 4 * G + t
                 nc.tensor.transpose(rb[:, t, :], rat[:, s : s + 1].to_broadcast([128, 128]), id_f32[:])
-            if half:
-                nc.vector.tensor_copy(out=rrow[:, 4 * half : 4 * half + 4, :], in_=rb[:])
+            if G:
+                nc.vector.tensor_copy(out=rrow[:, 4 * G : 4 * G + 4, :], in_=rb[:])
             else:
-                nc.scalar.copy(out=rrow[:, 4 * half : 4 * half + 4, :], in_=rb[:])
-
-        def scaled(engine, dst, src):
-            if engine == V:
-                nc.vector.tensor_scalar(dst, src, 0.03125, None, ALU.mult)
-            else:
-                nc.scalar.mul(dst, src, 0.03125)
+                nc.scalar.copy(out=rrow[:, 4 * G : 4 * G + 4, :], in_=rb[:])
 
         def moved(engine, dst, src):
             if engine == V:
@@ -116,327 +130,257 @@ def tile_multipleinputoperatorbranchtrunk_x1_kernel(
             else:
                 nc.scalar.copy(out=dst, in_=src)
 
-        def quantize(codes, scales, src):
+        def scaled(engine, dst, src):
+            if engine == V:
+                nc.vector.tensor_scalar(dst, src, 0.03125, None, ALU.mult)
+            else:
+                nc.scalar.mul(dst, src, 0.03125)
+
+        load = {V: 0.0, S: 0.0}
+
+        def quantize(codes, scales, src, columns):
+            load[V] += 12.0 + 0.22 * columns
             nc.vector.quantize_mx(out=codes.bitcast(FP8X4), scales=scales, in_=src)
 
+        ugs, wgs, cfs, b1s = {}, {}, {}, {}
 
-        uq, us, wq, ws = {}, {}, {}, {}
-        for i in range(2):
-            uq[i] = head.tile([128, 2, B], U32, name=f"uq{i}", align_bytes=64)
-            us[i] = head.tile([128, 2, B], U8, name=f"us{i}", align_bytes=64)
-            wq[i] = head.tile([128, 2, P], U32, name=f"wq{i}", align_bytes=64)
-            ws[i] = head.tile([128, 2, P], U8, name=f"ws{i}", align_bytes=64)
-        ugs, wgs, cfs = {}, {}, {}
-
-        def u_turn(i, g, half):
+        def turn(i, g, half):
             def job(engine):
                 if (g, half) == (0, 0):
                     ugs[i] = head.tile([128, 2, B, 4], BF16, name="ug", align_bytes=64)
-                words_out = ugs[i][:, g, :, :].rearrange("p r t -> p (r t)").bitcast(F32)
-                ut = ps.tile([128, 2, 256], F32, name="ut", tag="acc")
+                bank = ps.tile([128, 2, 256], F32, name="ut", tag="acc")
                 for r in range(2):
                     words = uraw[i][:, 2 * half + r, :].bitcast(F32)
                     for k in range(2):
                         nc.tensor.transpose(
-                            ut[:, k, 128 * r : 128 * (r + 1)],
+                            bank[:, k, 128 * r : 128 * (r + 1)],
                             words[:, 256 * g + k : 256 * (g + 1) : 2],
                             id_f32[:],
                         )
-                dst = words_out[:, 512 * half : 512 * (half + 1)].rearrange("p (r k) -> p r k", k=2)
-                src = ut[:].rearrange("p k r -> p r k")
-                moved(engine, dst, src)
-            return job
+                dst = ugs[i][:, g, 256 * half : 256 * (half + 1), :].rearrange("p r t -> p (r t)").bitcast(F32)
+                moved(engine, dst.rearrange("p (r k) -> p r k", k=2), bank[:].rearrange("p k r -> p r k"))
+                if (g, half) == (1, 1):
+                    later.append(lambda: quantize(
+                        uq[i][:].rearrange("p g b -> p (g b)"), us[i][:].rearrange("p g b -> p (g b)"),
+                        ugs[i][:].rearrange("p g r t -> p (g r t)"), 4096,
+                    ))
+            return (job, COST["bank"])
 
-        def u_quant(i):
+        def lay(i, g, t):
             def job(engine):
-                quantize(
-                    uq[i][:].rearrange("p g b -> p (g b)"), us[i][:].rearrange("p g b -> p (g b)"),
-                    ugs[i][:].rearrange("p g r t -> p (g r t)"),
+                if t == 0:
+                    wgs[i, g] = head.tile([128, 4 * P], BF16, name="wg", tag="wg", align_bytes=64, bufs=2)
+                moved(
+                    engine,
+                    wgs[i, g][:, 1024 * t : 1024 * (t + 1)].rearrange("p (i r j) -> p i j r", r=4, j=4),
+                    wraw[i, g][:].rearrange("p j (i t r) -> p t i j r", t=4, r=4)[:, t, :, :, :],
                 )
-            return job
-
-        def w_lay(i, g, half):
-            def job(engine):
-                if half == 0:
-                    wgs[i, g] = head.tile([128, 4 * P], BF16, name="wgt", tag="wg", align_bytes=64, bufs=2)
-                dst = wgs[i, g][:, 2048 * half : 2048 * (half + 1)].rearrange("p (t m j) -> p t m j", t=4, j=4)
-                src = wraw[i, g][:, :, 512 * half : 512 * (half + 1)].rearrange("p j (m t) -> p t m j", t=4)
-                moved(engine, dst, src)
-            return job
-
-        def w_quant(i, g):
-            def job(engine):
-                quantize(wq[i][:, g, :], ws[i][:, g, :], wgs[i, g][:])
-            return job
+                if t == 3:
+                    later.append(lambda: quantize(wq[i][:, g, :], ws[i][:, g, :], wgs[i, g][:], 4096))
+            return (job, COST["lay"])
 
         def branch(i, G, b):
-            acc = ps.tile([128, 4, 128], F32, name="br", tag="acc")
+            bank = ps.tile([128, 4, 128], F32, name="br", tag="acc")
             for t in range(4):
-                f = slice(512 * G + 128 * t, 512 * G + 128 * (t + 1))
+                f = slice(256 * t + 128 * G, 256 * t + 128 * (G + 1))
                 r = slice(128 * b, 128 * (b + 1))
                 for g in range(2):
                     nc.tensor.matmul_mx(
-                        out=acc[:, t, :],
+                        out=bank[:, t, :],
                         lhsT=wq[i][:, g, f].bitcast(FP8X4), lhsT_scale=ws[i][:, g, f],
                         rhs=uq[i][:, g, r].bitcast(FP8X4), rhs_scale=us[i][:, g, r],
                         start=(g == 0), stop=(g == 1),
                     )
-            return acc
+            return bank[:].rearrange("p t b -> p b t")
 
-        b1s = {}
-
-        def branch1(G, b):
+        def coef(k):
             def job(engine):
-                a1 = branch(0, G, b)
-                b1s[G, b] = head.tile([128, 128, 4], F32, name="b1", bufs=3)
-                nc.scalar.activation(out=b1s[G, b][:], in_=a1[:].rearrange("p t b -> p b t"), func=ACT.Tanh)
-            return job
+                flush()
+                if k < 8:
+                    G, b = divmod(k, 4)
+                    src = branch(0, G, b)
+                    b1s[k] = head.tile([128, 128, 4], F32, name="b1", bufs=3)
+                    nc.scalar.activation(out=b1s[k][:], in_=src, func=ACT.Tanh)
+                    load[S] += 450.0
+                if k >= 2:
+                    G, b = divmod(k - 2, 4)
+                    if b == 0:
+                        cfs[G] = head.tile([128, B, 4], BF16, name="cf", align_bytes=64)
+                    src = branch(1, G, b)
+                    nc.vector.tensor_tensor(cfs[G][:, 128 * b : 128 * (b + 1), :], src, b1s[k - 2][:], ALU.mult)
+                    load[V] += 440.0
+                    if b == 3:
+                        quantize(cq[:, G, :], cs[:, G, :], cfs[G][:].rearrange("p b t -> p (b t)"), 2048)
+                if k == 9:
+                    coef_ready.append(True)
+                    for h in chunks:
+                        add_rows(h)
+            return (job, {V: 0.0, S: 0.0})
 
-        def branch2(G, b):
+        outs, narrowed, planes = {}, {}, {}
+
+        def rows(h, bt):
             def job(engine):
-                if b == 0:
-                    cfs[G] = head.tile([128, B, 4], BF16, name="cf", align_bytes=64)
-                a2 = branch(1, G, b)
-                nc.vector.tensor_tensor(
-                    cfs[G][:, 128 * b : 128 * (b + 1), :], a2[:].rearrange("p t b -> p b t"), b1s[G, b][:], ALU.mult
-                )
-            return job
-
-        def coef_quant(G):
-            def job(engine):
-                quantize(cq[:, G, :], cs[:, G, :], cfs[G][:].rearrange("p b t -> p (b t)"))
-            return job
-
-        tiles = {}
-
-        def rows(bt, hh):
-            def job(engine):
-                bs = slice(128 * bt, 128 * (bt + 1))
                 if bt == 0:
-                    tiles[hh] = head.tile([128, 4, 512], F32, name="o", tag="wraw", bufs=3)
-                h = hh
-                acc = ps.tile([128, 512], F32, name="oa", tag="acc")
+                    outs[h] = head.tile([128, 4, 512], F32, name="o", tag="wraw", bufs=3)
+                bs = slice(128 * bt, 128 * (bt + 1))
+                bank = ps.tile([128, 512], F32, name="oa", tag="acc")
                 for G in range(2):
                     nc.tensor.matmul_mx(
-                        out=acc[:],
+                        out=bank[:],
                         lhsT=cq[:, G, bs].bitcast(FP8X4), lhsT_scale=cs[:, G, bs],
                         rhs=tq[:, h, G, :].bitcast(FP8X4), rhs_scale=ts[:, h, G, :],
                         start=(G == 0), stop=(G == 1),
                     )
-                scaled(
-                    engine,
-                    tiles[hh][:, bt, :].rearrange("b (p t) -> b p t", t=4),
-                    acc[:].rearrange("b (t p) -> b p t", t=4),
-                )
-                if bt % ROWS_PER_STORE == ROWS_PER_STORE - 1:
-                    b0 = bt + 1 - ROWS_PER_STORE
+                scaled(engine, outs[h][:, bt, :], bank[:])
+                if bt % 2 == 1:
+                    later.append(lambda: narrow(h, bt // 2))
                     nc.sync.dma_start(
-                        out=out_0[128 * b0 : 128 * (bt + 1), 512 * h : 512 * (h + 1)].rearrange("(b p) n -> p b n", p=128),
-                        in_=tiles[hh][:, b0 : bt + 1, :],
+                        out=out_0[128 * (bt - 1) : 128 * (bt + 1), 512 * h : 512 * (h + 1)].rearrange(
+                            "(b p) n -> p b n", p=128
+                        ),
+                        in_=outs[h][:, bt - 1 : bt + 1, :],
                     )
-            return job
+            return (job, COST["bank"])
 
-        def narrow(hh, pair):
+        def narrow(h, pair):
+            if pair == 0:
+                narrowed[h] = head.tile([128, 4, 512], BF16, name="ob", bufs=2)
+            engine = lighter(COST["narrow"])
+            moved(engine, narrowed[h][:, 2 * pair : 2 * pair + 2, :], outs[h][:, 2 * pair : 2 * pair + 2, :])
+            jobs.append(plane(h, pair))
+
+        def plane(h, pair):
             def job(engine):
                 if pair == 0:
-                    tiles["n", hh] = head.tile([128, 4, 512], BF16, name="ob", tag="ob", bufs=2)
-                dst = tiles["n", hh][:, 2 * pair : 2 * pair + 2, :]
-                src = tiles[hh][:, 2 * pair : 2 * pair + 2, :]
-                moved(engine, dst, src)
-            return job
-
-        def plane(hh, pair):
-            def job(engine):
-                if pair == 0:
-                    tiles["p", hh] = head.tile([128, B, 4], BF16, name="pl", align_bytes=64, tag="wg", bufs=2)
-                ut = ps.tile([128, 2, 256], F32, name="pt", tag="acc")
+                    planes[h] = head.tile([128, B, 4], BF16, name="pl", tag="wg", align_bytes=64, bufs=2)
+                bank = ps.tile([128, 2, 256], F32, name="pt", tag="acc")
                 for r in range(2):
-                    words = tiles["n", hh][:, 2 * pair + r, :].bitcast(F32)
+                    words = narrowed[h][:, 2 * pair + r, :].bitcast(F32)
                     for k in range(2):
-                        nc.tensor.transpose(ut[:, k, 128 * r : 128 * (r + 1)], words[:, k:256:2], id_f32[:])
-                dst = tiles["p", hh][:].rearrange("p b t -> p (b t)").bitcast(F32)
-                dst = dst[:, 512 * pair : 512 * (pair + 1)].rearrange("p (r k) -> p r k", k=2)
-                src = ut[:].rearrange("p k r -> p r k")
-                moved(engine, dst, src)
-            return job
+                        nc.tensor.transpose(bank[:, k, 128 * r : 128 * (r + 1)], words[:, k:256:2], id_f32[:])
+                dst = planes[h][:, 256 * pair : 256 * (pair + 1), :].rearrange("p r t -> p (r t)").bitcast(F32)
+                moved(engine, dst.rearrange("p (r k) -> p r k", k=2), bank[:].rearrange("p k r -> p r k"))
+                if pair == 1:
+                    later.append(lambda: store_planes(h))
+            return (job, COST["bank"])
 
-        def plane_quant(hh):
-            def job(engine):
-                h = hh
-                pq = head.tile([128, B], U32, name="pq", align_bytes=64, bufs=3)
-                pc = head.tile([128, B], U8, name="pc", align_bytes=64, bufs=3)
-                quantize(pq[:], pc[:], tiles["p", hh][:].rearrange("p b t -> p (b t)"))
+        def store_planes(h):
+            pq = head.tile([128, B], U32, name="pq", align_bytes=64, bufs=3)
+            pc = head.tile([128, B], U8, name="pc", align_bytes=64, bufs=3)
+            quantize(pq[:], pc[:], planes[h][:].rearrange("p b t -> p (b t)"), 2048)
+            nc.sync.dma_start(out=out_1[h].rearrange("p m t -> p (m t)").bitcast(I32), in_=pq[:].bitcast(I32))
+            for q in range(4):
                 nc.sync.dma_start(
-                    out=out_1[h].rearrange("p m t -> p (m t)").bitcast(I32), in_=pq[:].bitcast(I32)
-                )
-                for q in range(4):
-                    nc.sync.dma_start(
-                        out=out_2[h, 4 * q : 4 * q + 4, :].bitcast(I32),
-                        in_=pc[32 * q : 32 * q + 4, :].bitcast(I32),
-                    )
-            return job
-
-        lines, ths, grps = {}, {}, {}
-        block = [0]
-
-        def line(h, t):
-            lines[h, t] = work.tile([128, 8, 128], F32, name="line", bufs=6)
-            b = 4 * h + t
-            args = (lines[h, t][:], rrow[:], crd[:, b, 1:2], crd[:, b, 0:1], ALU.mult, ALU.add)
-            nc.vector.tensor_scalar(*args)
-
-        def feature(h, s):
-            g, t = divmod(s, 4)
-            if t == 0:
-                ths[h, g] = work.tile([128, 4, 512], F32, name="th", bufs=4)
-            pres = []
-            for f in range(2):
-                pre = ps_x.tile([128, 4, 128], F32, name="pre")
-                for b in range(4):
-                    nc.tensor.transpose(pre[:, b, :], lines[h, b][:, s + f, :], id_f32[:])
-                pres.append(pre)
-            for f in range(2):
-                nc.scalar.activation(
-                    out=ths[h, g][:, t + f, :], in_=pres[f][:].rearrange("p b n -> p (b n)"), func=ACT.Tanh,
-                    scale=w0s[:, s + f : s + f + 1], bias=par[:, 2, s + f : s + f + 1],
+                    out=out_2[h, 4 * q : 4 * q + 4, :].bitcast(I32), in_=pc[32 * q : 32 * q + 4, :].bitcast(I32)
                 )
 
-        def gain_block(h, g, b):
-            if h not in grps:
-                grps[h] = work.tile([128, 2, 512, 4], BF16, name="grp", align_bytes=64, bufs=1)
-            src = ths[h, g][:, :, 128 * b : 128 * (b + 1)].rearrange("p t n -> p n t")
-            dst = grps[h][:, g, 128 * b : 128 * (b + 1), :]
-            if 4 * g + b >= GAIN_ON_GPSIMD:
-                nc.vector.tensor_tensor(
-                    dst, src, prm[:, 4 * g : 4 * g + 4, 3].unsqueeze(1).to_broadcast([128, 128, 4]), ALU.mult
-                )
-            else:
-                nc.gpsimd.tensor_tensor(
-                    dst, src, par[:, 3, 4 * g : 4 * g + 4].unsqueeze(1).to_broadcast([128, 128, 4]), ALU.mult
-                )
-
-        def trunk_quant(h):
-            quantize(
-                tq[:, h, :, :].rearrange("p g n -> p (g n)"), ts[:, h, :, :].rearrange("p g n -> p (g n)"),
-                grps[h][:].rearrange("p g n t -> p (g n t)"),
-            )
-
-        def each(*fns):
-            for fn in fns:
-                fn()
-
-        load = {V: 0.0, S: 0.0}
-        todo = []
-        locked = []
+        jobs, later, coef_ready, chunks = [], [], [], []
         credit = [0.0]
 
-        def add(job, cost_v, cost_s, only=None, then=()):
-            todo.append((job, {V: cost_v, S: cost_s}, only, then))
+        def lighter(cost):
+            engine = V if load[V] + cost[V] <= load[S] + cost[S] else S
+            load[engine] += cost[engine]
+            return engine
 
         def run(amount):
             credit[0] += amount
-            while todo and credit[0] > 0.0:
-                job, cost, only, then = todo[0]
-                todo.remove(todo[0])
-                engine = only
-                if engine is None:
-                    engine = V if load[V] + cost[V] <= load[S] + cost[S] else S
+            while jobs and credit[0] > 0.0:
+                job, cost = jobs[0]
+                jobs.remove(jobs[0])
+                engine = lighter(cost)
                 job(engine)
-                load[engine] += cost[engine]
                 credit[0] -= cost[engine]
-                locked.extend(then)
-
-        def quant(fn, cols):
-            load[V] += 12 + 0.22 * cols
-            fn(V)
-
-        def add_rows(h):
-            for bt in range(4):
-                add(rows(bt, h), 440, 445, then=((narrow_then_plane, h, bt // 2),) if bt % 2 == 1 else ())
-
-        def narrow_then_plane(h, pair):
-            engine = V if load[V] + 460 <= load[S] + NARROW_S else S
-            load[engine] += {V: 460, S: 870}[engine]
-            narrow(h, pair)(engine)
-            add(plane(h, pair), 440, 445, then=((quant, plane_quant(h), 2048),) if pair else ())
 
         def flush():
-            now = locked[:]
-            locked.clear()
-            for fn, *args in now:
-                fn(*args)
+            now = later[:]
+            later.clear()
+            for fn in now:
+                fn()
 
-        def lay(i, g, half):
-            add(w_lay(i, g, half), 1050, LAY_S, then=((quant, w_quant(i, g), 4096),) if half else ())
+        def add_rows(h):
+            jobs.extend([rows(h, bt) for bt in range(4)])
 
-        def turn(i):
-            for g in range(2):
-                for half in range(2):
-                    add(u_turn(i, g, half), 440, 445, then=((quant, u_quant(i), 4096),) if (g, half) == (1, 1) else ())
+        halves = [(g, half) for g in range(2) for half in range(2)]
+        jobs.extend([lay(0, 0, t) for t in range(4)])
+        jobs.extend([turn(0, g, half) for g, half in halves])
+        jobs.extend([lay(0, 1, t) for t in range(4)])
+        jobs.extend([turn(1, g, half) for g, half in halves])
+        jobs.extend([lay(1, g, t) for g in range(2) for t in range(4)])
+        jobs.extend([coef(k) for k in range(10)])
 
-        order = [(G, b) for G in range(2) for b in range(4)]
-        chunks_done = []
-        coef_done = []
+        lines, ths, grps = {}, {}, {}
 
-        def coef_end():
-            quant(coef_quant(0), 2048)
-            quant(coef_quant(1), 2048)
-            coef_done.append(True)
-            for h in chunks_done:
+        def line(h, t):
+            lines[h, t] = work.tile([128, 8, 128], F32, name="line", bufs=6)
+            k = 4 * h + t
+            args = (lines[h, t][:], rrow[:], xy[:, 1, k : k + 1], xy[:, 0, k : k + 1], ALU.mult, ALU.add)
+            if h > 0 and t < LINES_ON_GPSIMD:
+                nc.gpsimd.tensor_scalar(*args)
+            else:
+                nc.vector.tensor_scalar(*args)
+                load[V] += 440.0
+
+        def features(h, s):
+            G, t = divmod(s, 4)
+            if t == 0:
+                ths[h, G] = work.tile([128, 4, 512], F32, name="th", bufs=4)
+            banks = []
+            for f in range(s, s + 2):
+                pre = ps_x.tile([128, 4, 128], F32, name="pre")
+                for b in range(4):
+                    nc.tensor.transpose(pre[:, b, :], lines[h, b][:, f, :], id_f32[:])
+                banks.append(pre)
+            for f in range(2):
+                nc.scalar.activation(
+                    out=ths[h, G][:, t + f, :], in_=banks[f][:].rearrange("p b n -> p (b n)"), func=ACT.Tanh,
+                    scale=w0s[:, s + f : s + f + 1], bias=par[:, 2, s + f : s + f + 1],
+                )
+            load[S] += 940.0
+
+        def gains(h):
+            grps[h] = work.tile([128, 2, 512, 4], BF16, name="grp", align_bytes=64, bufs=1)
+            for k in range(8):
+                G, b = divmod(k, 4)
+                cols = slice(128 * b, 128 * (b + 1))
+                dst, src = grps[h][:, G, cols, :], ths[h, G][:, :, cols]
+                if k < GAIN_ON_GPSIMD:
+                    nc.gpsimd.tensor_tensor(
+                        dst, src.rearrange("p t n -> p n t"),
+                        par[:, 3, 4 * G : 4 * G + 4].unsqueeze(1).to_broadcast([128, 128, 4]), ALU.mult,
+                    )
+                else:
+                    nc.vector.tensor_tensor(
+                        dst.rearrange("p (c i) t -> p c t i", i=4), src.rearrange("p t (c i) -> p c t i", i=4),
+                        prm[:, 4 * G : 4 * G + 4, 3].unsqueeze(1).unsqueeze(3).to_broadcast([128, 32, 4, 4]), ALU.mult,
+                    )
+                    load[V] += 440.0
+
+        def trunk_codes(h):
+            quantize(
+                tq[:, h, :, :].rearrange("p g n -> p (g n)"), ts[:, h, :, :].rearrange("p g n -> p (g n)"),
+                grps[h][:].rearrange("p g n t -> p (g n t)"), 4096,
+            )
+            chunks.append(h)
+            if coef_ready:
                 add_rows(h)
 
         for t in range(4):
             line(0, t)
-        load[V] += 1760
-        lay(0, 0, 0)
-        lay(0, 0, 1)
-        turn(0)
-        lay(0, 1, 0)
-        lay(0, 1, 1)
-        turn(1)
-        lay(1, 0, 0)
-        lay(1, 0, 1)
-        lay(1, 1, 0)
-        lay(1, 1, 1)
-
-        def pair_job(k):
-            def job(engine):
-                flush()
-                if k < 8:
-                    branch1(*order[k])(S)
-                    load[S] += 470
-                if k >= 2:
-                    branch2(*order[k - 2])(V)
-                    load[V] += 440
-            return job
-
-        for k in range(10):
-            add(pair_job(k), 0, 0, only=V, then=((coef_end,),) if k == 9 else ())
-
-        first = (3000.0, 9000.0)
-        run(first[0])
-        for h in range(10):
+        run(FIRST_BUDGET)
+        for h in range(8 + LAG_QUANT):
             if h < 7:
                 for t in range(4):
                     line(h + 1, t)
-                load[V] += 1760
-            rate = (first[1] if not coef_done else 5000.0) / 4
             for s in range(0, 8, 2):
                 if h < 8:
-                    feature(h, s)
-                    load[S] += 940
-                run(rate)
+                    features(h, s)
+                run((OUT_BUDGET if coef_ready else HEAD_BUDGET) / 4)
                 flush()
-            if 2 <= h < 10:
-                quant(lambda engine: trunk_quant(h - 2), 4096)
-                chunks_done.append(h - 2)
-                if coef_done:
-                    add_rows(h - 2)
-            if 1 <= h < 9:
-                for g in range(2):
-                    for b in range(4):
-                        gain_block(h - 1, g, b)
-                load[V] += 440 * (8 - GAIN_ON_GPSIMD)
-        while todo or locked:
+            if h >= LAG_QUANT:
+                trunk_codes(h - LAG_QUANT)
+            if 0 <= h - LAG_GAIN < 8:
+                gains(h - LAG_GAIN)
+        while jobs or later:
             run(900.0)
             flush()

@@ -16,20 +16,84 @@ ALU = mybir.AluOpType
 ACT = mybir.ActivationFunctionType
 
 TINY = 2.0 ** -60
-V, S = "vector", "scalar"
-
+T, V, S, G = "tensor", "vector", "scalar", "gpsimd"
+GAIN_EITHER = 3
 GAIN_ON_GPSIMD = 3
-LINES_ON_GPSIMD = 0
-LAG_GAIN = 1
-LAG_QUANT = 2
-FIRST_BUDGET = 3000.0
-HEAD_BUDGET = 9000.0
-OUT_BUDGET = 5000.0
-COST = {
-    "bank": {V: 440.0, S: 445.0},
-    "lay": {V: 530.0, S: 1000.0},
-    "narrow": {V: 440.0, S: 870.0},
-}
+RINGS = {"acc": 4, "pre": 3, "line": 8, "th": 3, "grp": 1, "wg": 2, "ug": 1, "raw": 5, "b1": 3, "cf": 1, "ob": 2, "pq": 3, "pc": 3}
+LATENCY = 150
+SLOW = 1
+SWITCH = 60
+
+
+def plan(ops, arrivals):
+    writers, users, rings, room = {}, {}, {}, {}
+    needs = []
+    for k, (where, weight, reads, writes, shared_port, emit) in enumerate(ops):
+        need = []
+        for token in reads:
+            need += writers.get(token, [])
+        for token in writes:
+            if token not in users:
+                ring = rings.setdefault(token[0], [])
+                ring.append(token)
+                depth = RINGS.get(token[0], 0)
+                room[token] = list(users[ring[-1 - depth]]) if depth and len(ring) > depth else []
+            need += room[token]
+        for token in reads:
+            users.setdefault(token, []).append(k)
+        for token in writes:
+            users.setdefault(token, []).append(k)
+            writers.setdefault(token, []).append(k)
+        needs.append(set(need))
+    rank = [0] * len(ops)
+    for k in reversed(range(len(ops))):
+        weight = ops[k][1]
+        rank[k] += min(weight) if isinstance(weight, tuple) else weight
+        for d in needs[k]:
+            rank[d] = max(rank[d], rank[k] + LATENCY)
+    finish, engine_of, free, order = {}, {}, {T: 0, V: 0, S: 0, G: 0}, []
+    port_free, port_owner, last_kind = 0, None, None
+    left = list(range(len(ops)))
+    while left:
+        best = None
+        for engine in (T, V, S, G):
+            chosen = None
+            seen = 0
+            for k in left:
+                where, weight, reads, writes, shared_port, emit = ops[k]
+                if engine not in where:
+                    continue
+                if any(d not in finish for d in needs[k]):
+                    continue
+                start = free[engine]
+                for token in reads:
+                    start = max(start, arrivals.get(token, 0))
+                for d in needs[k]:
+                    wait = 0 if engine_of[d] == engine == T else 180 if engine_of[d] == engine else LATENCY
+                    start = max(start, finish[d] + wait)
+                uses_port = shared_port or engine == G
+                if uses_port and engine in (V, G) and port_owner != engine:
+                    start = max(start, port_free)
+                key = (start + (150 if engine == G and V in where else 0), -rank[k])
+                if chosen is None or key < chosen[2]:
+                    chosen = (start, k, key)
+            if chosen and (best is None or chosen[2][0] < best[3]):
+                best = (chosen[0], engine, chosen[1], chosen[2][0])
+        start, engine, k, key = best
+        where, weight, reads, writes, shared_port, emit = ops[k]
+        length = weight[where.index(engine)] if isinstance(weight, tuple) else weight
+        if engine == T:
+            kind = writes[0][0] == "pre" or writes[0][-1] == "turn"
+            length = length * SLOW + (SWITCH if kind != last_kind else 0)
+            last_kind = kind
+        finish[k] = start + length
+        engine_of[k] = engine
+        free[engine] = finish[k]
+        if (shared_port or engine == G) and engine in (V, G):
+            port_free, port_owner = finish[k], engine
+        left.remove(k)
+        order.append((k, engine))
+    return order
 
 
 def tile_multipleinputoperatorbranchtrunk_x1_kernel(
@@ -41,31 +105,36 @@ def tile_multipleinputoperatorbranchtrunk_x1_kernel(
         work = ctx.enter_context(tc.tile_pool(name="work", bufs=2))
         head = ctx.enter_context(tc.tile_pool(name="head", bufs=1))
         ps_fix = ctx.enter_context(tc.psum_pool(name="ps_fix", bufs=1))
-        ps_x = ctx.enter_context(tc.psum_pool(name="ps_x", bufs=3))
-        ps = ctx.enter_context(tc.psum_pool(name="ps", bufs=4))
+        ps_x = ctx.enter_context(tc.psum_pool(name="ps_x", bufs=RINGS["pre"]))
+        ps = ctx.enter_context(tc.psum_pool(name="ps", bufs=RINGS["acc"]))
+        ctx.enter_context(tc.manual_schedule())
 
         small = keep.tile([128, P], BF16, name="small")
         nc.vector.memset(small[:], 0.0)
-        wraw = {}
+        wraw, uraw = {}, {}
 
         def load_w(i, g, w):
-            wraw[i, g] = head.tile([128, 4, P], BF16, name="wr", tag="wraw", bufs=3)
+            wraw[i, g] = head.tile([128, 4, P], BF16, name="wr", tag="raw", bufs=RINGS["raw"])
             nc.sync.dma_start(
                 out=wraw[i, g][:], in_=w[512 * g : 512 * (g + 1), :].rearrange("(p j) c -> p j c", j=4)
             )
 
-        nc.sync.dma_start(out=small[0:3, :], in_=wt)
-        nc.sync.dma_start(out=small[3:4, :], in_=gain.unsqueeze(0))
-        nc.sync.dma_start(out=small[32:64, 0:256], in_=coords.rearrange("(k p) c -> k (p c)", p=128))
-        load_w(0, 0, w1)
-        uraw = {}
-        for i, u in ((0, u1), (1, u2)):
-            uraw[i] = head.tile([128, 4, M], BF16, name=f"uraw{i}")
+        def load_u(i, u):
+            uraw[i] = head.tile([128, 4, M], BF16, name="ur", tag="raw", bufs=RINGS["raw"])
             nc.sync.dma_start(out=uraw[i][:], in_=u.rearrange("(b p) m -> p b m", p=128))
-            if i == 0:
-                load_w(0, 1, w1)
+
+        nc.scalar.dma_start(out=small[0:3, :], in_=wt)
+        nc.scalar.dma_start(out=small[3:4, :], in_=gain.unsqueeze(0))
+        nc.scalar.dma_start(out=small[32:64, 0:256], in_=coords.rearrange("(k p) c -> k (p c)", p=128))
+        load_w(0, 0, w1)
+        load_u(0, u1)
+        load_w(0, 1, w1)
+        load_u(1, u2)
         load_w(1, 0, w2)
-        load_w(1, 1, w2)
+
+        arrivals = {("small",): 3300}
+        for k, token in enumerate([("wraw", 0, 0), ("uraw", 0), ("wraw", 0, 1), ("uraw", 1), ("wraw", 1, 0), ("wraw", 1, 1)]):
+            arrivals[token] = 5000 + 2150 * k
 
         id_bf = keep.tile([128, 128], BF16, name="id_bf")
         make_identity(nc, id_bf[:])
@@ -76,6 +145,15 @@ def tile_multipleinputoperatorbranchtrunk_x1_kernel(
         ts = keep.tile([128, 8, 2, 512], U8, name="ts", align_bytes=64)
         cq = keep.tile([128, 2, B], U32, name="cq", align_bytes=64)
         cs = keep.tile([128, 2, B], U8, name="cs", align_bytes=64)
+        turned = keep.tile([128, P], BF16, name="turned")
+        xy = keep.tile([128, 2, 32], F32, name="xy")
+        par = keep.tile([128, 4, 8], F32, name="par")
+        w0s = keep.tile([128, 8], F32, name="w0s")
+        rat = keep.tile([128, 8], F32, name="rat")
+        tmpa = keep.tile([128, 8], F32, name="tmpa")
+        tmpb = keep.tile([128, 8], F32, name="tmpb")
+        rrow = keep.tile([128, 8, 128], F32, name="rrow")
+        prm = ps_fix.tile([128, 8, 128], BF16, name="prm")
         uq, us, wq, ws = {}, {}, {}, {}
         for i in range(2):
             uq[i] = head.tile([128, 2, B], U32, name=f"uq{i}", align_bytes=64)
@@ -83,46 +161,19 @@ def tile_multipleinputoperatorbranchtrunk_x1_kernel(
             wq[i] = head.tile([128, 2, P], U32, name=f"wq{i}", align_bytes=64)
             ws[i] = head.tile([128, 2, P], U8, name=f"ws{i}", align_bytes=64)
 
-        turned = keep.tile([128, P], BF16, name="turned")
-        nc.vector.tensor_copy(
-            out=turned[:].rearrange("p (t i r) -> p t i r", t=4, r=4),
-            in_=small[:].rearrange("p (i t r) -> p t i r", t=4, r=4),
-        )
-        xy = keep.tile([128, 2, 32], F32, name="xy")
-        xyp = ps.tile([128, 2, 128], BF16, name="xyp", tag="acc")
-        for c in range(2):
-            nc.tensor.transpose(xyp[:, c, :], small[:, c:256:2], id_bf[:])
-        prm = ps_fix.tile([128, 8, 128], BF16, name="prm")
-        for s in range(8):
-            G, t = divmod(s, 4)
-            col = 256 * t + 128 * G
-            nc.tensor.transpose(prm[:, s, :], turned[:, col : col + 128], id_bf[:])
-        par = keep.tile([128, 4, 8], F32, name="par")
-        w0s = keep.tile([128, 8], F32, name="w0s")
-        rat = keep.tile([128, 8], F32, name="rat")
-        tmpa = keep.tile([128, 8], F32, name="tmpa")
-        tmpb = keep.tile([128, 8], F32, name="tmpb")
-        nc.vector.tensor_copy(out=par[:].rearrange("p v s -> p s v"), in_=prm[:, :, 0:4])
-        nc.scalar.copy(out=xy[:], in_=xyp[:, :, 32:64])
-        nc.vector.tensor_single_scalar(tmpa[:], par[:, 0, :], TINY, ALU.is_lt)
-        nc.vector.scalar_tensor_tensor(
-            out=tmpb[:], in0=par[:, 0, :], scalar=-TINY, in1=tmpa[:], op0=ALU.is_gt, op1=ALU.mult
-        )
-        nc.vector.scalar_tensor_tensor(
-            out=w0s[:], in0=tmpb[:], scalar=2.0 * TINY, in1=par[:, 0, :], op0=ALU.mult, op1=ALU.add
-        )
-        nc.vector.reciprocal(tmpa[:], w0s[:])
-        nc.vector.tensor_mul(rat[:], tmpa[:], par[:, 1, :])
-        rrow = keep.tile([128, 8, 128], F32, name="rrow")
-        for G in range(2):
-            rb = ps.tile([128, 4, 128], F32, name="rb", tag="acc")
-            for t in range(4):
-                s = 4 * G + t
-                nc.tensor.transpose(rb[:, t, :], rat[:, s : s + 1].to_broadcast([128, 128]), id_f32[:])
-            if G:
-                nc.vector.tensor_copy(out=rrow[:, 4 * G : 4 * G + 4, :], in_=rb[:])
-            else:
-                nc.scalar.copy(out=rrow[:, 4 * G : 4 * G + 4, :], in_=rb[:])
+        ops, copied = [], {}
+        tiles = {}
+
+        def op(where, weight, reads, writes, emit, shared_port=False):
+            ops.append((where, weight, reads, writes, shared_port, emit))
+
+        def fresh(pool, token, shape, dtype, tag=None, align_bytes=0):
+            if token not in tiles:
+                extra = {"align_bytes": align_bytes} if align_bytes else {}
+                tiles[token] = pool.tile(
+                    shape, dtype, name=token[0], tag=tag or token[0], bufs=RINGS[tag or token[0]], **extra
+                )
+            return tiles[token]
 
         def moved(engine, dst, src):
             if engine == V:
@@ -136,251 +187,308 @@ def tile_multipleinputoperatorbranchtrunk_x1_kernel(
             else:
                 nc.scalar.mul(dst, src, 0.03125)
 
-        load = {V: 0.0, S: 0.0}
-
-        def quantize(codes, scales, src, columns):
-            load[V] += 12.0 + 0.22 * columns
+        def quantize(codes, scales, src):
             nc.vector.quantize_mx(out=codes.bitcast(FP8X4), scales=scales, in_=src)
 
-        ugs, wgs, cfs, b1s = {}, {}, {}, {}
+        BANK = (528, 525)
 
-        def turn(i, g, half):
-            def job(engine):
-                if (g, half) == (0, 0):
-                    ugs[i] = head.tile([128, 2, B, 4], BF16, name="ug", align_bytes=64)
-                bank = ps.tile([128, 2, 256], F32, name="ut", tag="acc")
+        def turn_rows(engine):
+            nc.vector.tensor_copy(
+                out=turned[:].rearrange("p (t i r) -> p t i r", t=4, r=4),
+                in_=small[:].rearrange("p (i t r) -> p t i r", t=4, r=4),
+            )
+
+        def turn_xy(engine):
+            bank = fresh(ps, ("acc", "xy"), [128, 2, 128], BF16, "acc")
+            for c in range(2):
+                nc.tensor.transpose(bank[:, c, :], small[:, c:256:2], id_bf[:])
+
+        def turn_params(engine):
+            for s in range(8):
+                g, t = divmod(s, 4)
+                col = 256 * t + 128 * g
+                nc.tensor.transpose(prm[:, s, :], turned[:, col : col + 128], id_bf[:])
+
+        def ratios(engine):
+            nc.vector.tensor_copy(out=par[:].rearrange("p v s -> p s v"), in_=prm[:, :, 0:4])
+            nc.vector.tensor_single_scalar(tmpa[:], par[:, 0, :], TINY, ALU.is_lt)
+            nc.vector.scalar_tensor_tensor(
+                out=tmpb[:], in0=par[:, 0, :], scalar=-TINY, in1=tmpa[:], op0=ALU.is_gt, op1=ALU.mult
+            )
+            nc.vector.scalar_tensor_tensor(
+                out=w0s[:], in0=tmpb[:], scalar=2.0 * TINY, in1=par[:, 0, :], op0=ALU.mult, op1=ALU.add
+            )
+            nc.vector.reciprocal(tmpa[:], w0s[:])
+            nc.vector.tensor_mul(rat[:], tmpa[:], par[:, 1, :])
+
+        op((V,), 300, [("small",)], [("turned",)], turn_rows)
+        op((T,), 128, [("small",)], [("acc", "xy", "turn")], turn_xy)
+        op((S,), 90, [("acc", "xy", "turn")], [("xy",)], lambda engine: nc.scalar.copy(out=xy[:], in_=tiles["acc", "xy"][:, :, 32:64]))
+        op((T,), 500, [("turned",)], [("prm", "turn")], turn_params)
+        op((V,), 1300, [("prm", "turn")], [("rat",)], ratios)
+
+        def spread(g):
+            def emit(engine):
+                bank = fresh(ps, ("acc", "r", g), [128, 4, 128], F32, "acc")
+                for t in range(4):
+                    s = 4 * g + t
+                    nc.tensor.transpose(bank[:, t, :], rat[:, s : s + 1].to_broadcast([128, 128]), id_f32[:])
+            op((T,), 310, [("rat",)], [("acc", "r", g, "turn")], emit)
+            op((V, S), BANK, [("acc", "r", g, "turn")], [("rrow",)],
+               lambda engine: moved(engine, rrow[:, 4 * g : 4 * g + 4, :], tiles["acc", "r", g][:]))
+
+        spread(0)
+        spread(1)
+
+        def turn_u(i, g, half):
+            def transposes(engine):
+                bank = fresh(ps, ("acc", "u", i, g, half), [128, 2, 256], F32, "acc")
                 for r in range(2):
                     words = uraw[i][:, 2 * half + r, :].bitcast(F32)
                     for k in range(2):
                         nc.tensor.transpose(
-                            bank[:, k, 128 * r : 128 * (r + 1)],
-                            words[:, 256 * g + k : 256 * (g + 1) : 2],
-                            id_f32[:],
+                            bank[:, k, 128 * r : 128 * (r + 1)], words[:, 256 * g + k : 256 * (g + 1) : 2], id_f32[:]
                         )
-                dst = ugs[i][:, g, 256 * half : 256 * (half + 1), :].rearrange("p r t -> p (r t)").bitcast(F32)
-                moved(engine, dst.rearrange("p (r k) -> p r k", k=2), bank[:].rearrange("p k r -> p r k"))
-                if (g, half) == (1, 1):
-                    later.append(lambda: quantize(
-                        uq[i][:].rearrange("p g b -> p (g b)"), us[i][:].rearrange("p g b -> p (g b)"),
-                        ugs[i][:].rearrange("p g r t -> p (g r t)"), 4096,
-                    ))
-            return (job, COST["bank"])
+
+            def copy(engine):
+                ug = fresh(head, ("ug", i), [128, 2, B, 4], BF16, align_bytes=64)
+                dst = ug[:, g, 256 * half : 256 * (half + 1), :].rearrange("p r t -> p (r t)").bitcast(F32)
+                moved(engine, dst.rearrange("p (r k) -> p r k", k=2),
+                      tiles["acc", "u", i, g, half][:].rearrange("p k r -> p r k"))
+
+            bank = ("acc", "u", i, g, half, "turn")
+            op((T,), 504, [("uraw", i)], [bank], transposes)
+            op((V, S), BANK, [bank], [("ug", i)], copy)
+
+        def codes_u(i):
+            op((V,), 1100, [("ug", i)], [("uq", i)], lambda engine: quantize(
+                uq[i][:].rearrange("p g b -> p (g b)"), us[i][:].rearrange("p g b -> p (g b)"),
+                tiles["ug", i][:].rearrange("p g r t -> p (g r t)")), True)
 
         def lay(i, g, t):
-            def job(engine):
-                if t == 0:
-                    wgs[i, g] = head.tile([128, 4 * P], BF16, name="wg", tag="wg", align_bytes=64, bufs=2)
+            def emit(engine):
+                if (i, g) not in wraw:
+                    load_w(i, g, w2)
+                wg = fresh(head, ("wg", i, g), [128, 4 * P], BF16, align_bytes=64)
                 moved(
                     engine,
-                    wgs[i, g][:, 1024 * t : 1024 * (t + 1)].rearrange("p (i r j) -> p i j r", r=4, j=4),
+                    wg[:, 1024 * t : 1024 * (t + 1)].rearrange("p (i r j) -> p i j r", r=4, j=4),
                     wraw[i, g][:].rearrange("p j (i t r) -> p t i j r", t=4, r=4)[:, t, :, :, :],
                 )
-                if t == 3:
-                    later.append(lambda: quantize(wq[i][:, g, :], ws[i][:, g, :], wgs[i, g][:], 4096))
-            return (job, COST["lay"])
+            op((V, S), (640, 1300), [("wraw", i, g)], [("wg", i, g)], emit, True)
 
-        def branch(i, G, b):
-            bank = ps.tile([128, 4, 128], F32, name="br", tag="acc")
-            for t in range(4):
-                f = slice(256 * t + 128 * G, 256 * t + 128 * (G + 1))
+        def codes_w(i, g):
+            def emit(engine):
+                quantize(wq[i][:, g, :], ws[i][:, g, :], tiles["wg", i, g][:])
+                if (i, g) == (0, 0):
+                    load_w(1, 1, w2)
+            op((V,), 1100, [("wg", i, g)], [("wq", i, g)], emit, True)
+
+        def branch(i, g, b):
+            def emit(engine):
+                bank = fresh(ps, ("acc", "b", i, g, b), [128, 4, 128], F32, "acc")
                 r = slice(128 * b, 128 * (b + 1))
-                for g in range(2):
-                    nc.tensor.matmul_mx(
-                        out=bank[:, t, :],
-                        lhsT=wq[i][:, g, f].bitcast(FP8X4), lhsT_scale=ws[i][:, g, f],
-                        rhs=uq[i][:, g, r].bitcast(FP8X4), rhs_scale=us[i][:, g, r],
-                        start=(g == 0), stop=(g == 1),
-                    )
-            return bank[:].rearrange("p t b -> p b t")
+                for t in range(4):
+                    f = slice(256 * t + 128 * g, 256 * t + 128 * (g + 1))
+                    for k in range(2):
+                        nc.tensor.matmul_mx(
+                            out=bank[:, t, :],
+                            lhsT=wq[i][:, k, f].bitcast(FP8X4), lhsT_scale=ws[i][:, k, f],
+                            rhs=uq[i][:, k, r].bitcast(FP8X4), rhs_scale=us[i][:, k, r],
+                            start=(k == 0), stop=(k == 1),
+                        )
+            op((T,), 600, [("wq", i, 0), ("wq", i, 1), ("uq", i)], [("acc", "b", i, g, b)], emit)
 
-        def coef(k):
-            def job(engine):
-                flush()
-                if k < 8:
-                    G, b = divmod(k, 4)
-                    src = branch(0, G, b)
-                    b1s[k] = head.tile([128, 128, 4], F32, name="b1", bufs=3)
-                    nc.scalar.activation(out=b1s[k][:], in_=src, func=ACT.Tanh)
-                    load[S] += 450.0
-                if k >= 2:
-                    G, b = divmod(k - 2, 4)
-                    if b == 0:
-                        cfs[G] = head.tile([128, B, 4], BF16, name="cf", align_bytes=64)
-                    src = branch(1, G, b)
-                    nc.vector.tensor_tensor(cfs[G][:, 128 * b : 128 * (b + 1), :], src, b1s[k - 2][:], ALU.mult)
-                    load[V] += 440.0
-                    if b == 3:
-                        quantize(cq[:, G, :], cs[:, G, :], cfs[G][:].rearrange("p b t -> p (b t)"), 2048)
-                if k == 9:
-                    coef_ready.append(True)
-                    for h in chunks:
-                        add_rows(h)
-            return (job, {V: 0.0, S: 0.0})
+        def coef(g, b):
+            def first(engine):
+                b1 = fresh(head, ("b1", g, b), [128, 128, 4], F32)
+                nc.scalar.activation(
+                    out=b1[:], in_=tiles["acc", "b", 0, g, b][:].rearrange("p t b -> p b t"), func=ACT.Tanh
+                )
 
-        outs, narrowed, planes = {}, {}, {}
+            def product(engine):
+                cf = fresh(head, ("cf", g), [128, B, 4], BF16, align_bytes=64)
+                nc.vector.tensor_tensor(
+                    cf[:, 128 * b : 128 * (b + 1), :], tiles["acc", "b", 1, g, b][:].rearrange("p t b -> p b t"),
+                    tiles["b1", g, b][:], ALU.mult,
+                )
+
+            branch(0, g, b)
+            op((S,), 540, [("acc", "b", 0, g, b)], [("b1", g, b)], first)
+            branch(1, g, b)
+            op((V,), 528, [("acc", "b", 1, g, b), ("b1", g, b)], [("cf", g)], product)
+
+        def codes_coef(g):
+            op((V,), 560, [("cf", g)], [("cq", g)], lambda engine: quantize(
+                cq[:, g, :], cs[:, g, :], tiles["cf", g][:].rearrange("p b t -> p (b t)")), True)
 
         def rows(h, bt):
-            def job(engine):
-                if bt == 0:
-                    outs[h] = head.tile([128, 4, 512], F32, name="o", tag="wraw", bufs=3)
-                bs = slice(128 * bt, 128 * (bt + 1))
-                bank = ps.tile([128, 512], F32, name="oa", tag="acc")
-                for G in range(2):
+            bs = slice(128 * bt, 128 * (bt + 1))
+
+            def product(engine):
+                bank = fresh(ps, ("acc", "o", h, bt), [128, 512], F32, "acc")
+                for g in range(2):
                     nc.tensor.matmul_mx(
                         out=bank[:],
-                        lhsT=cq[:, G, bs].bitcast(FP8X4), lhsT_scale=cs[:, G, bs],
-                        rhs=tq[:, h, G, :].bitcast(FP8X4), rhs_scale=ts[:, h, G, :],
-                        start=(G == 0), stop=(G == 1),
+                        lhsT=cq[:, g, bs].bitcast(FP8X4), lhsT_scale=cs[:, g, bs],
+                        rhs=tq[:, h, g, :].bitcast(FP8X4), rhs_scale=ts[:, h, g, :],
+                        start=(g == 0), stop=(g == 1),
                     )
-                scaled(engine, outs[h][:, bt, :], bank[:])
-                if bt % 2 == 1:
-                    later.append(lambda: narrow(h, bt // 2))
+
+            def copy(engine):
+                out = fresh(head, ("raw", h), [128, 4, 512], F32)
+                scaled(engine, out[:, bt, :], tiles["acc", "o", h, bt][:])
+                b0 = bt - bt % 2
+                copied[h, b0] = copied.get((h, b0), 0) + 1
+                if copied[h, b0] == 2:
                     nc.sync.dma_start(
-                        out=out_0[128 * (bt - 1) : 128 * (bt + 1), 512 * h : 512 * (h + 1)].rearrange(
+                        out=out_0[128 * b0 : 128 * (b0 + 2), 512 * h : 512 * (h + 1)].rearrange(
                             "(b p) n -> p b n", p=128
                         ),
-                        in_=outs[h][:, bt - 1 : bt + 1, :],
+                        in_=out[:, b0 : b0 + 2, :],
                     )
-            return (job, COST["bank"])
+
+            op((T,), 534, [("cq", 0), ("cq", 1), ("tq", h)], [("acc", "o", h, bt)], product)
+            op((V, S), BANK, [("acc", "o", h, bt)], [("raw", h), ("pair", h, bt // 2)], copy)
 
         def narrow(h, pair):
-            if pair == 0:
-                narrowed[h] = head.tile([128, 4, 512], BF16, name="ob", bufs=2)
-            engine = lighter(COST["narrow"])
-            moved(engine, narrowed[h][:, 2 * pair : 2 * pair + 2, :], outs[h][:, 2 * pair : 2 * pair + 2, :])
-            jobs.append(plane(h, pair))
+            both = slice(2 * pair, 2 * pair + 2)
 
-        def plane(h, pair):
-            def job(engine):
-                if pair == 0:
-                    planes[h] = head.tile([128, B, 4], BF16, name="pl", tag="wg", align_bytes=64, bufs=2)
-                bank = ps.tile([128, 2, 256], F32, name="pt", tag="acc")
+            def copy(engine):
+                ob = fresh(head, ("ob", h), [128, 4, 512], BF16)
+                moved(engine, ob[:, both, :], tiles["raw", h][:, both, :])
+
+            def transposes(engine):
+                bank = fresh(ps, ("acc", "p", h, pair), [128, 2, 256], F32, "acc")
                 for r in range(2):
-                    words = narrowed[h][:, 2 * pair + r, :].bitcast(F32)
+                    words = tiles["ob", h][:, 2 * pair + r, :].bitcast(F32)
                     for k in range(2):
                         nc.tensor.transpose(bank[:, k, 128 * r : 128 * (r + 1)], words[:, k:256:2], id_f32[:])
-                dst = planes[h][:, 256 * pair : 256 * (pair + 1), :].rearrange("p r t -> p (r t)").bitcast(F32)
-                moved(engine, dst.rearrange("p (r k) -> p r k", k=2), bank[:].rearrange("p k r -> p r k"))
-                if pair == 1:
-                    later.append(lambda: store_planes(h))
-            return (job, COST["bank"])
+
+            def back(engine):
+                pl = fresh(head, ("wg", "p", h), [128, B, 4], BF16, "wg", align_bytes=64)
+                dst = pl[:, 256 * pair : 256 * (pair + 1), :].rearrange("p r t -> p (r t)").bitcast(F32)
+                moved(engine, dst.rearrange("p (r k) -> p r k", k=2),
+                      tiles["acc", "p", h, pair][:].rearrange("p k r -> p r k"))
+
+            op((V, S), (530, 1045), [("pair", h, pair)], [("ob", h), ("half", h, pair)], copy, True)
+            bank = ("acc", "p", h, pair, "turn")
+            op((T,), 504, [("half", h, pair)], [bank], transposes)
+            op((V, S), BANK, [bank], [("wg", "p", h)], back)
 
         def store_planes(h):
-            pq = head.tile([128, B], U32, name="pq", align_bytes=64, bufs=3)
-            pc = head.tile([128, B], U8, name="pc", align_bytes=64, bufs=3)
-            quantize(pq[:], pc[:], planes[h][:].rearrange("p b t -> p (b t)"), 2048)
-            nc.sync.dma_start(out=out_1[h].rearrange("p m t -> p (m t)").bitcast(I32), in_=pq[:].bitcast(I32))
-            for q in range(4):
-                nc.sync.dma_start(
-                    out=out_2[h, 4 * q : 4 * q + 4, :].bitcast(I32), in_=pc[32 * q : 32 * q + 4, :].bitcast(I32)
+            def emit(engine):
+                pq = fresh(head, ("pq", h), [128, B], U32, align_bytes=64)
+                pc = fresh(head, ("pc", h), [128, B], U8, "pc", align_bytes=64)
+                quantize(pq[:], pc[:], tiles["wg", "p", h][:].rearrange("p b t -> p (b t)"))
+                nc.sync.dma_start(out=out_1[h].rearrange("p m t -> p (m t)").bitcast(I32), in_=pq[:].bitcast(I32))
+                for q in range(4):
+                    nc.sync.dma_start(
+                        out=out_2[h, 4 * q : 4 * q + 4, :].bitcast(I32), in_=pc[32 * q : 32 * q + 4, :].bitcast(I32)
+                    )
+            op((V,), 560, [("wg", "p", h)], [("pq", h)], emit, True)
+
+        def line(h, b):
+            def emit(engine):
+                k = 4 * h + b
+                nc.vector.tensor_scalar(
+                    fresh(work, ("line", h, b), [128, 8, 128], F32)[:], rrow[:],
+                    xy[:, 1, k : k + 1], xy[:, 0, k : k + 1], ALU.mult, ALU.add,
                 )
-
-        jobs, later, coef_ready, chunks = [], [], [], []
-        credit = [0.0]
-
-        def lighter(cost):
-            engine = V if load[V] + cost[V] <= load[S] + cost[S] else S
-            load[engine] += cost[engine]
-            return engine
-
-        def run(amount):
-            credit[0] += amount
-            while jobs and credit[0] > 0.0:
-                job, cost = jobs[0]
-                jobs.remove(jobs[0])
-                engine = lighter(cost)
-                job(engine)
-                credit[0] -= cost[engine]
-
-        def flush():
-            now = later[:]
-            later.clear()
-            for fn in now:
-                fn()
-
-        def add_rows(h):
-            jobs.extend([rows(h, bt) for bt in range(4)])
-
-        halves = [(g, half) for g in range(2) for half in range(2)]
-        jobs.extend([lay(0, 0, t) for t in range(4)])
-        jobs.extend([turn(0, g, half) for g, half in halves])
-        jobs.extend([lay(0, 1, t) for t in range(4)])
-        jobs.extend([turn(1, g, half) for g, half in halves])
-        jobs.extend([lay(1, g, t) for g in range(2) for t in range(4)])
-        jobs.extend([coef(k) for k in range(10)])
-
-        lines, ths, grps = {}, {}, {}
-
-        def line(h, t):
-            lines[h, t] = work.tile([128, 8, 128], F32, name="line", bufs=6)
-            k = 4 * h + t
-            args = (lines[h, t][:], rrow[:], xy[:, 1, k : k + 1], xy[:, 0, k : k + 1], ALU.mult, ALU.add)
-            if h > 0 and t < LINES_ON_GPSIMD:
-                nc.gpsimd.tensor_scalar(*args)
-            else:
-                nc.vector.tensor_scalar(*args)
-                load[V] += 440.0
+            op((V,), 530, [("rrow",), ("xy",)], [("line", h, b)], emit, True)
 
         def features(h, s):
-            G, t = divmod(s, 4)
-            if t == 0:
-                ths[h, G] = work.tile([128, 4, 512], F32, name="th", bufs=4)
-            banks = []
-            for f in range(s, s + 2):
-                pre = ps_x.tile([128, 4, 128], F32, name="pre")
-                for b in range(4):
-                    nc.tensor.transpose(pre[:, b, :], lines[h, b][:, f, :], id_f32[:])
-                banks.append(pre)
-            for f in range(2):
-                nc.scalar.activation(
-                    out=ths[h, G][:, t + f, :], in_=banks[f][:].rearrange("p b n -> p (b n)"), func=ACT.Tanh,
-                    scale=w0s[:, s + f : s + f + 1], bias=par[:, 2, s + f : s + f + 1],
-                )
-            load[S] += 940.0
+            g, t = divmod(s, 4)
 
-        def gains(h):
-            grps[h] = work.tile([128, 2, 512, 4], BF16, name="grp", align_bytes=64, bufs=1)
-            for k in range(8):
-                G, b = divmod(k, 4)
-                cols = slice(128 * b, 128 * (b + 1))
-                dst, src = grps[h][:, G, cols, :], ths[h, G][:, :, cols]
-                if k < GAIN_ON_GPSIMD:
+            def transposes(engine):
+                for f in range(s, s + 2):
+                    pre = fresh(ps_x, ("pre", h, f), [128, 4, 128], F32)
+                    for b in range(4):
+                        nc.tensor.transpose(pre[:, b, :], tiles["line", h, b][:, f, :], id_f32[:])
+
+            def tanh(f):
+                def emit(engine):
+                    th = fresh(work, ("th", h, g), [128, 4, 512], F32)
+                    nc.scalar.activation(
+                        out=th[:, f - 4 * g, :], in_=tiles["pre", h, f][:].rearrange("p b n -> p (b n)"),
+                        func=ACT.Tanh, scale=w0s[:, f : f + 1], bias=par[:, 2, f : f + 1],
+                    )
+                op((S,), 560, [("pre", h, f)], [("th", h, g)], emit)
+
+            op((T,), 616, [("line", h, b) for b in range(4)], [("pre", h, s), ("pre", h, s + 1)], transposes)
+            tanh(s)
+            tanh(s + 1)
+
+        def gain_block(h, k):
+            g, b = divmod(k, 4)
+            cols = slice(128 * b, 128 * (b + 1))
+
+            def emit(engine):
+                grp = fresh(work, ("grp", h), [128, 2, 512, 4], BF16, align_bytes=64)
+                dst, src = grp[:, g, cols, :], tiles["th", h, g][:, :, cols]
+                if engine == G:
                     nc.gpsimd.tensor_tensor(
                         dst, src.rearrange("p t n -> p n t"),
-                        par[:, 3, 4 * G : 4 * G + 4].unsqueeze(1).to_broadcast([128, 128, 4]), ALU.mult,
+                        par[:, 3, 4 * g : 4 * g + 4].unsqueeze(1).to_broadcast([128, 128, 4]), ALU.mult,
                     )
                 else:
                     nc.vector.tensor_tensor(
                         dst.rearrange("p (c i) t -> p c t i", i=4), src.rearrange("p t (c i) -> p c t i", i=4),
-                        prm[:, 4 * G : 4 * G + 4, 3].unsqueeze(1).unsqueeze(3).to_broadcast([128, 32, 4, 4]), ALU.mult,
+                        prm[:, 4 * g : 4 * g + 4, 3].unsqueeze(1).unsqueeze(3).to_broadcast([128, 32, 4, 4]), ALU.mult,
                     )
-                    load[V] += 440.0
 
-        def trunk_codes(h):
-            quantize(
+            if k < GAIN_ON_GPSIMD:
+                op((G,), 1130, [("th", h, g)], [("grp", h)], emit, True)
+            elif k < GAIN_EITHER:
+                op((V, G), (540, 1130), [("th", h, g)], [("grp", h)], emit)
+            else:
+                op((V,), 540, [("th", h, g)], [("grp", h)], emit)
+
+        def codes_trunk(h):
+            op((V,), 1100, [("grp", h)], [("tq", h)], lambda engine: quantize(
                 tq[:, h, :, :].rearrange("p g n -> p (g n)"), ts[:, h, :, :].rearrange("p g n -> p (g n)"),
-                grps[h][:].rearrange("p g n t -> p (g n t)"), 4096,
-            )
-            chunks.append(h)
-            if coef_ready:
-                add_rows(h)
+                tiles["grp", h][:].rearrange("p g n t -> p (g n t)")), True)
 
-        for t in range(4):
-            line(0, t)
-        run(FIRST_BUDGET)
-        for h in range(8 + LAG_QUANT):
-            if h < 7:
-                for t in range(4):
-                    line(h + 1, t)
+        def branches():
+            for i in range(2):
+                for g in range(2):
+                    for t in range(4):
+                        lay(i, g, t)
+                    codes_w(i, g)
+                    for half in range(2):
+                        turn_u(i, g, half)
+                codes_u(i)
+            for g in range(2):
+                for b in range(4):
+                    coef(g, b)
+                codes_coef(g)
+
+        def trunk(h):
+            for b in range(4):
+                line(h, b)
             for s in range(0, 8, 2):
-                if h < 8:
-                    features(h, s)
-                run((OUT_BUDGET if coef_ready else HEAD_BUDGET) / 4)
-                flush()
-            if h >= LAG_QUANT:
-                trunk_codes(h - LAG_QUANT)
-            if 0 <= h - LAG_GAIN < 8:
-                gains(h - LAG_GAIN)
-        while jobs or later:
-            run(900.0)
-            flush()
+                features(h, s)
+            for k in range(8):
+                gain_block(h, k)
+            codes_trunk(h)
+
+        def results(h):
+            rows(h, 0)
+            rows(h, 1)
+            narrow(h, 0)
+            rows(h, 2)
+            rows(h, 3)
+            narrow(h, 1)
+            store_planes(h)
+
+        trunk(0)
+        branches()
+        trunk(1)
+        for h in range(2, 8):
+            trunk(h)
+            results(h - 2)
+        results(6)
+        results(7)
+
+        for k, engine in plan(ops, arrivals):
+            ops[k][5](engine)

@@ -15,84 +15,108 @@ FP8X4 = mybir.dt.float8_e4m3fn_x4
 ALU = mybir.AluOpType
 ACT = mybir.ActivationFunctionType
 
+CHUNKS = N // 512
 TINY = 2.0 ** -60
-T, V, S, G = "tensor", "vector", "scalar", "gpsimd"
-GAIN_EITHER = 3
-GAIN_ON_GPSIMD = 3
-RINGS = {"acc": 4, "pre": 3, "line": 8, "th": 3, "grp": 1, "wg": 2, "ug": 1, "raw": 5, "b1": 3, "cf": 1, "ob": 2, "pq": 3, "pc": 3}
-LATENCY = 150
-SLOW = 1
-SWITCH = 60
+
+TENSOR, VECTOR, SCALAR, GPSIMD = "tensor", "vector", "scalar", "gpsimd"
+
+GAIN_ON_GPSIMD = (0, 3, 6)
+
+DEPTH = {
+    "bank": 4,
+    "pre": 3,
+    "line": 8,
+    "th": 3,
+    "grp": 1,
+    "wide": 2,
+    "ug": 1,
+    "raw": 5,
+    "b1": 3, "cf": 1,
+    "ob": 2,
+    "pq": 3, "pc": 3,
+}
+
+COPY = 540
+TANH, TANH_BRANCH = 580, 540
+GAIN, GAIN_GPSIMD = 540, 1130
+LINE = 530
+NARROW = {VECTOR: 530, SCALAR: 1045}
+LAY = {VECTOR: 600, SCALAR: 1250}
+CODES = 1140
+SORT, SAMPLES, DIVIDE = 300, 90, 1300
+PASS, BRANCH = 267, 600
+TURN = 77
+TURN_STEPPED = 160
+SWITCH = 96
+HANDOVER = 170
+OWN_RESULT = 180
+SMALL_LOADED = 3300
+FIRST_LOADED, NEXT_LOADED = 5000, 2150
 
 
-def plan(ops, arrivals):
-    writers, users, rings, room = {}, {}, {}, {}
-    needs = []
-    for k, (where, weight, reads, writes, shared_port, emit) in enumerate(ops):
+def plan(work):
+    writers, users, opened, room, needs = {}, {}, {}, {}, []
+    for k, (engines, lengths, reads, writes, port, turns, emit) in enumerate(work):
         need = []
         for token in reads:
             need += writers.get(token, [])
         for token in writes:
-            if token not in users:
-                ring = rings.setdefault(token[0], [])
-                ring.append(token)
-                depth = RINGS.get(token[0], 0)
-                room[token] = list(users[ring[-1 - depth]]) if depth and len(ring) > depth else []
+            if token not in room:
+                row = opened.setdefault(token[0], [])
+                row.append(token)
+                depth = DEPTH.get(token[0], 0)
+                room[token] = list(users[row[-1 - depth]]) if depth and len(row) > depth else []
             need += room[token]
-        for token in reads:
+        for token in reads + writes:
             users.setdefault(token, []).append(k)
         for token in writes:
-            users.setdefault(token, []).append(k)
             writers.setdefault(token, []).append(k)
         needs.append(set(need))
-    rank = [0] * len(ops)
-    for k in reversed(range(len(ops))):
-        weight = ops[k][1]
-        rank[k] += min(weight) if isinstance(weight, tuple) else weight
+
+    rank = [0] * len(work)
+    for k in reversed(range(len(work))):
+        rank[k] += min(work[k][1])
         for d in needs[k]:
-            rank[d] = max(rank[d], rank[k] + LATENCY)
-    finish, engine_of, free, order = {}, {}, {T: 0, V: 0, S: 0, G: 0}, []
-    port_free, port_owner, last_kind = 0, None, None
-    left = list(range(len(ops)))
+            rank[d] = max(rank[d], rank[k] + HANDOVER)
+
+    loads = [("w", 0, 0), ("u", 0), ("w", 0, 1), ("u", 1), ("w", 1, 0), ("w", 1, 1)]
+    loaded = {token: FIRST_LOADED + NEXT_LOADED * k for k, token in enumerate(loads)}
+    loaded[("small",)] = SMALL_LOADED
+    free = {TENSOR: 0, VECTOR: 0, SCALAR: 0, GPSIMD: 0}
+    finish, runs_on, order = {}, {}, []
+    port_free, port_owner, turned = 0, None, None
+    left = list(range(len(work)))
     while left:
-        best = None
-        for engine in (T, V, S, G):
-            chosen = None
-            seen = 0
+        candidates = []
+        for engine in free:
+            options = []
             for k in left:
-                where, weight, reads, writes, shared_port, emit = ops[k]
-                if engine not in where:
+                engines, lengths, reads, writes, port, turns, emit = work[k]
+                if engine not in engines or any(d not in finish for d in needs[k]):
                     continue
-                if any(d not in finish for d in needs[k]):
-                    continue
-                start = free[engine]
-                for token in reads:
-                    start = max(start, arrivals.get(token, 0))
+                asked = max([free[engine]] + [loaded.get(token, 0) for token in reads])
                 for d in needs[k]:
-                    wait = 0 if engine_of[d] == engine == T else 180 if engine_of[d] == engine else LATENCY
-                    start = max(start, finish[d] + wait)
-                uses_port = shared_port or engine == G
-                if uses_port and engine in (V, G) and port_owner != engine:
-                    start = max(start, port_free)
-                key = (start + (150 if engine == G and V in where else 0), -rank[k])
-                if chosen is None or key < chosen[2]:
-                    chosen = (start, k, key)
-            if chosen and (best is None or chosen[2][0] < best[3]):
-                best = (chosen[0], engine, chosen[1], chosen[2][0])
-        start, engine, k, key = best
-        where, weight, reads, writes, shared_port, emit = ops[k]
-        length = weight[where.index(engine)] if isinstance(weight, tuple) else weight
-        if engine == T:
-            kind = writes[0][0] == "pre" or writes[0][-1] == "turn"
-            length = length * SLOW + (SWITCH if kind != last_kind else 0)
-            last_kind = kind
-        finish[k] = start + length
-        engine_of[k] = engine
+                    if runs_on[d] != engine:
+                        asked = max(asked, finish[d] + HANDOVER)
+                    elif engine != TENSOR:
+                        asked = max(asked, finish[d] + OWN_RESULT)
+                held = port and engine in (VECTOR, GPSIMD) and port_owner != engine
+                options.append((max(asked, port_free) if held else asked, -rank[k], asked, k))
+            if options:
+                start, urgency, asked, k = min(options)
+                candidates.append((start, asked, engine, k))
+        start, asked, engine, k = min(candidates)
+        engines, lengths, reads, writes, port, turns, emit = work[k]
+        finish[k] = start + lengths[engines.index(engine)]
+        if engine == TENSOR and turns != turned:
+            finish[k] += SWITCH
+            turned = turns
         free[engine] = finish[k]
-        if (shared_port or engine == G) and engine in (V, G):
+        runs_on[k] = engine
+        if port and engine in (VECTOR, GPSIMD):
             port_free, port_owner = finish[k], engine
         left.remove(k)
-        order.append((k, engine))
+        order.append((emit, engine))
     return order
 
 
@@ -102,331 +126,276 @@ def tile_multipleinputoperatorbranchtrunk_x1_kernel(
     nc = tc.nc
     with ExitStack() as ctx:
         keep = ctx.enter_context(tc.tile_pool(name="keep", bufs=1))
-        work = ctx.enter_context(tc.tile_pool(name="work", bufs=2))
-        head = ctx.enter_context(tc.tile_pool(name="head", bufs=1))
-        ps_fix = ctx.enter_context(tc.psum_pool(name="ps_fix", bufs=1))
-        ps_x = ctx.enter_context(tc.psum_pool(name="ps_x", bufs=RINGS["pre"]))
-        ps = ctx.enter_context(tc.psum_pool(name="ps", bufs=RINGS["acc"]))
+        ring = ctx.enter_context(tc.tile_pool(name="ring", bufs=1))
+        psum_keep = ctx.enter_context(tc.psum_pool(name="psum_keep", bufs=1))
+        psum = ctx.enter_context(tc.psum_pool(name="psum", bufs=1))
         ctx.enter_context(tc.manual_schedule())
 
         small = keep.tile([128, P], BF16, name="small")
-        nc.vector.memset(small[:], 0.0)
-        wraw, uraw = {}, {}
-
-        def load_w(i, g, w):
-            wraw[i, g] = head.tile([128, 4, P], BF16, name="wr", tag="raw", bufs=RINGS["raw"])
-            nc.sync.dma_start(
-                out=wraw[i, g][:], in_=w[512 * g : 512 * (g + 1), :].rearrange("(p j) c -> p j c", j=4)
-            )
-
-        def load_u(i, u):
-            uraw[i] = head.tile([128, 4, M], BF16, name="ur", tag="raw", bufs=RINGS["raw"])
-            nc.sync.dma_start(out=uraw[i][:], in_=u.rearrange("(b p) m -> p b m", p=128))
-
+        nc.gpsimd.memset(small[:].bitcast(I32), 0)
         nc.scalar.dma_start(out=small[0:3, :], in_=wt)
         nc.scalar.dma_start(out=small[3:4, :], in_=gain.unsqueeze(0))
         nc.scalar.dma_start(out=small[32:64, 0:256], in_=coords.rearrange("(k p) c -> k (p c)", p=128))
-        load_w(0, 0, w1)
-        load_u(0, u1)
-        load_w(0, 1, w1)
-        load_u(1, u2)
-        load_w(1, 0, w2)
 
-        arrivals = {("small",): 3300}
-        for k, token in enumerate([("wraw", 0, 0), ("uraw", 0), ("wraw", 0, 1), ("uraw", 1), ("wraw", 1, 0), ("wraw", 1, 1)]):
-            arrivals[token] = 5000 + 2150 * k
+        raw = {}
 
-        id_bf = keep.tile([128, 128], BF16, name="id_bf")
-        make_identity(nc, id_bf[:])
+        def load_w(i, g):
+            raw["w", i, g] = ring.tile([128, 4, P], BF16, name="w_raw", tag="raw", bufs=DEPTH["raw"])
+            rows = (w1, w2)[i][512 * g : 512 * (g + 1), :]
+            nc.sync.dma_start(out=raw["w", i, g][:], in_=rows.rearrange("(p j) c -> p j c", j=4))
+
+        def load_u(i):
+            raw["u", i] = ring.tile([128, 4, M], BF16, name="u_raw", tag="raw", bufs=DEPTH["raw"])
+            nc.sync.dma_start(out=raw["u", i][:], in_=(u1, u2)[i].rearrange("(b p) m -> p b m", p=128))
+
+        load_w(0, 0)
+        load_u(0)
+        load_w(0, 1)
+        load_u(1)
+        load_w(1, 0)
+
+        id_bf16 = keep.tile([128, 128], BF16, name="id_bf16")
+        make_identity(nc, id_bf16[:])
         id_f32 = keep.tile([128, 128], F32, name="id_f32")
         make_identity(nc, id_f32[:])
 
-        tq = keep.tile([128, 8, 2, 512], U32, name="tq", align_bytes=64)
-        ts = keep.tile([128, 8, 2, 512], U8, name="ts", align_bytes=64)
-        cq = keep.tile([128, 2, B], U32, name="cq", align_bytes=64)
-        cs = keep.tile([128, 2, B], U8, name="cs", align_bytes=64)
-        turned = keep.tile([128, P], BF16, name="turned")
+        trunk_q = keep.tile([128, CHUNKS, 2, 512], U32, name="trunk_q", align_bytes=64)
+        trunk_s = keep.tile([128, CHUNKS, 2, 512], U8, name="trunk_s", align_bytes=64)
+        coef_q = keep.tile([128, 2, B], U32, name="coef_q", align_bytes=64)
+        coef_s = keep.tile([128, 2, B], U8, name="coef_s", align_bytes=64)
+        u_q, u_s, w_q, w_s = {}, {}, {}, {}
+        for i in range(2):
+            u_q[i] = keep.tile([128, 2, B], U32, name=f"u_q{i}", align_bytes=64)
+            u_s[i] = keep.tile([128, 2, B], U8, name=f"u_s{i}", align_bytes=64)
+            w_q[i] = keep.tile([128, 2, P], U32, name=f"w_q{i}", align_bytes=64)
+            w_s[i] = keep.tile([128, 2, P], U8, name=f"w_s{i}", align_bytes=64)
+        sorted_rows = keep.tile([128, P], BF16, name="sorted_rows")
         xy = keep.tile([128, 2, 32], F32, name="xy")
         par = keep.tile([128, 4, 8], F32, name="par")
-        w0s = keep.tile([128, 8], F32, name="w0s")
-        rat = keep.tile([128, 8], F32, name="rat")
-        tmpa = keep.tile([128, 8], F32, name="tmpa")
-        tmpb = keep.tile([128, 8], F32, name="tmpb")
-        rrow = keep.tile([128, 8, 128], F32, name="rrow")
-        prm = ps_fix.tile([128, 8, 128], BF16, name="prm")
-        uq, us, wq, ws = {}, {}, {}, {}
-        for i in range(2):
-            uq[i] = head.tile([128, 2, B], U32, name=f"uq{i}", align_bytes=64)
-            us[i] = head.tile([128, 2, B], U8, name=f"us{i}", align_bytes=64)
-            wq[i] = head.tile([128, 2, P], U32, name=f"wq{i}", align_bytes=64)
-            ws[i] = head.tile([128, 2, P], U8, name=f"ws{i}", align_bytes=64)
+        w0 = keep.tile([128, 8], F32, name="w0")
+        ratio = keep.tile([128, 8], F32, name="ratio")
+        tmp_a = keep.tile([128, 8], F32, name="tmp_a")
+        tmp_b = keep.tile([128, 8], F32, name="tmp_b")
+        ratio_row = keep.tile([128, 8, 128], F32, name="ratio_row")
+        par_bank = psum_keep.tile([128, 8, 128], BF16, name="par_bank")
 
-        ops, copied = [], {}
-        tiles = {}
+        work, tiles, stored = [], {}, {}
 
-        def op(where, weight, reads, writes, emit, shared_port=False):
-            ops.append((where, weight, reads, writes, shared_port, emit))
+        def add(lengths, reads, writes, emit, port=False, turns=False):
+            work.append((tuple(lengths), tuple(lengths.values()), reads, writes, port, turns, emit))
 
-        def fresh(pool, token, shape, dtype, tag=None, align_bytes=0):
+        def tile(token, shape, dtype, align_bytes=0, pool=ring):
             if token not in tiles:
-                extra = {"align_bytes": align_bytes} if align_bytes else {}
+                more = {"align_bytes": align_bytes} if align_bytes else {}
                 tiles[token] = pool.tile(
-                    shape, dtype, name=token[0], tag=tag or token[0], bufs=RINGS[tag or token[0]], **extra
+                    shape, dtype, name=token[0], tag=token[0], bufs=DEPTH[token[0]], **more
                 )
             return tiles[token]
 
+        def bank(token, shape, dtype=F32):
+            return tile(token, shape, dtype, pool=psum)
+
         def moved(engine, dst, src):
-            if engine == V:
+            if engine == VECTOR:
                 nc.vector.tensor_copy(out=dst, in_=src)
             else:
                 nc.scalar.copy(out=dst, in_=src)
 
-        def scaled(engine, dst, src):
-            if engine == V:
-                nc.vector.tensor_scalar(dst, src, 0.03125, None, ALU.mult)
-            else:
-                nc.scalar.mul(dst, src, 0.03125)
-
-        def quantize(codes, scales, src):
+        def quantized(codes, scales, src):
             nc.vector.quantize_mx(out=codes.bitcast(FP8X4), scales=scales, in_=src)
 
-        BANK = (528, 525)
+        def product(out, left, left_s, right, right_s):
+            for g in range(2):
+                nc.tensor.matmul_mx(
+                    out=out,
+                    lhsT=left[g].bitcast(FP8X4), lhsT_scale=left_s[g],
+                    rhs=right[g].bitcast(FP8X4), rhs_scale=right_s[g],
+                    start=(g == 0), stop=(g == 1),
+                )
 
-        def turn_rows(engine):
+        def word_turns(out, words):
+            for r in range(2):
+                for k in range(2):
+                    nc.tensor.transpose(out[:, k, 128 * r : 128 * (r + 1)], words(r)[:, k:256:2], id_f32[:])
+
+        def words_back(engine, dst, src):
+            dst = dst.rearrange("p r t -> p (r t)").bitcast(F32)
+            moved(engine, dst.rearrange("p (r k) -> p r k", k=2), src.rearrange("p k r -> p r k"))
+
+        both_copy = {VECTOR: COPY, SCALAR: COPY}
+
+        def sort_features(engine):
             nc.vector.tensor_copy(
-                out=turned[:].rearrange("p (t i r) -> p t i r", t=4, r=4),
+                out=sorted_rows[:].rearrange("p (t i r) -> p t i r", t=4, r=4),
                 in_=small[:].rearrange("p (i t r) -> p t i r", t=4, r=4),
             )
 
-        def turn_xy(engine):
-            bank = fresh(ps, ("acc", "xy"), [128, 2, 128], BF16, "acc")
+        def turn_samples(engine):
             for c in range(2):
-                nc.tensor.transpose(bank[:, c, :], small[:, c:256:2], id_bf[:])
+                nc.tensor.transpose(
+                    bank(("bank", "xy"), [128, 2, 128], BF16)[:, c, :], small[:, c:256:2], id_bf16[:]
+                )
 
-        def turn_params(engine):
+        def turn_parameters(engine):
             for s in range(8):
                 g, t = divmod(s, 4)
-                col = 256 * t + 128 * g
-                nc.tensor.transpose(prm[:, s, :], turned[:, col : col + 128], id_bf[:])
+                column = 256 * t + 128 * g
+                nc.tensor.transpose(par_bank[:, s, :], sorted_rows[:, column : column + 128], id_bf16[:])
 
-        def ratios(engine):
-            nc.vector.tensor_copy(out=par[:].rearrange("p v s -> p s v"), in_=prm[:, :, 0:4])
-            nc.vector.tensor_single_scalar(tmpa[:], par[:, 0, :], TINY, ALU.is_lt)
+        def divide(engine):
+            nc.vector.tensor_copy(out=par[:].rearrange("p v s -> p s v"), in_=par_bank[:, :, 0:4])
+            nc.vector.tensor_single_scalar(tmp_a[:], par[:, 0, :], TINY, ALU.is_lt)
             nc.vector.scalar_tensor_tensor(
-                out=tmpb[:], in0=par[:, 0, :], scalar=-TINY, in1=tmpa[:], op0=ALU.is_gt, op1=ALU.mult
+                out=tmp_b[:], in0=par[:, 0, :], scalar=-TINY, in1=tmp_a[:], op0=ALU.is_gt, op1=ALU.mult
             )
             nc.vector.scalar_tensor_tensor(
-                out=w0s[:], in0=tmpb[:], scalar=2.0 * TINY, in1=par[:, 0, :], op0=ALU.mult, op1=ALU.add
+                out=w0[:], in0=tmp_b[:], scalar=2.0 * TINY, in1=par[:, 0, :], op0=ALU.mult, op1=ALU.add
             )
-            nc.vector.reciprocal(tmpa[:], w0s[:])
-            nc.vector.tensor_mul(rat[:], tmpa[:], par[:, 1, :])
+            nc.vector.reciprocal(tmp_a[:], w0[:])
+            nc.vector.tensor_mul(ratio[:], tmp_a[:], par[:, 1, :])
 
-        op((V,), 300, [("small",)], [("turned",)], turn_rows)
-        op((T,), 128, [("small",)], [("acc", "xy", "turn")], turn_xy)
-        op((S,), 90, [("acc", "xy", "turn")], [("xy",)], lambda engine: nc.scalar.copy(out=xy[:], in_=tiles["acc", "xy"][:, :, 32:64]))
-        op((T,), 500, [("turned",)], [("prm", "turn")], turn_params)
-        op((V,), 1300, [("prm", "turn")], [("rat",)], ratios)
+        def parameters():
+            add({VECTOR: SORT}, [("small",)], [("sorted",)], sort_features)
+            add({TENSOR: 2 * TURN}, [("small",)], [("bank", "xy")], turn_samples, turns=True)
+            add({SCALAR: SAMPLES}, [("bank", "xy")], [("xy",)],
+                lambda engine: nc.scalar.copy(out=xy[:], in_=tiles["bank", "xy"][:, :, 32:64]))
+            add({TENSOR: 8 * TURN}, [("sorted",)], [("par",)], turn_parameters, turns=True)
+            add({VECTOR: DIVIDE}, [("par",)], [("ratio",)], divide)
+            for g in range(2):
+                ratio_row_half(g)
 
-        def spread(g):
-            def emit(engine):
-                bank = fresh(ps, ("acc", "r", g), [128, 4, 128], F32, "acc")
+        def ratio_row_half(g):
+            def turn(engine):
                 for t in range(4):
-                    s = 4 * g + t
-                    nc.tensor.transpose(bank[:, t, :], rat[:, s : s + 1].to_broadcast([128, 128]), id_f32[:])
-            op((T,), 310, [("rat",)], [("acc", "r", g, "turn")], emit)
-            op((V, S), BANK, [("acc", "r", g, "turn")], [("rrow",)],
-               lambda engine: moved(engine, rrow[:, 4 * g : 4 * g + 4, :], tiles["acc", "r", g][:]))
-
-        spread(0)
-        spread(1)
-
-        def turn_u(i, g, half):
-            def transposes(engine):
-                bank = fresh(ps, ("acc", "u", i, g, half), [128, 2, 256], F32, "acc")
-                for r in range(2):
-                    words = uraw[i][:, 2 * half + r, :].bitcast(F32)
-                    for k in range(2):
-                        nc.tensor.transpose(
-                            bank[:, k, 128 * r : 128 * (r + 1)], words[:, 256 * g + k : 256 * (g + 1) : 2], id_f32[:]
-                        )
+                    nc.tensor.transpose(
+                        bank(("bank", "r", g), [128, 4, 128])[:, t, :],
+                        ratio[:, 4 * g + t : 4 * g + t + 1].to_broadcast([128, 128]), id_f32[:],
+                    )
 
             def copy(engine):
-                ug = fresh(head, ("ug", i), [128, 2, B, 4], BF16, align_bytes=64)
-                dst = ug[:, g, 256 * half : 256 * (half + 1), :].rearrange("p r t -> p (r t)").bitcast(F32)
-                moved(engine, dst.rearrange("p (r k) -> p r k", k=2),
-                      tiles["acc", "u", i, g, half][:].rearrange("p k r -> p r k"))
+                moved(engine, ratio_row[:, 4 * g : 4 * g + 4, :], tiles["bank", "r", g][:])
 
-            bank = ("acc", "u", i, g, half, "turn")
-            op((T,), 504, [("uraw", i)], [bank], transposes)
-            op((V, S), BANK, [bank], [("ug", i)], copy)
+            add({TENSOR: 4 * TURN}, [("ratio",)], [("bank", "r", g)], turn, turns=True)
+            add(both_copy, [("bank", "r", g)], [("ratio_row",)], copy)
+
+        def turn_u(i, g, half):
+            def turn(engine):
+                out = bank(("bank", "u", i, g, half), [128, 2, 256])
+                word_turns(
+                    out, lambda r: raw["u", i][:, 2 * half + r, 512 * g : 512 * (g + 1)].bitcast(F32)
+                )
+
+            def copy(engine):
+                ug = tile(("ug", i), [128, 2, B, 4], BF16, 64)
+                words_back(engine, ug[:, g, 256 * half : 256 * (half + 1), :], tiles["bank", "u", i, g, half][:])
+
+            add({TENSOR: 4 * TURN_STEPPED}, [("u", i)], [("bank", "u", i, g, half)], turn, turns=True)
+            add(both_copy, [("bank", "u", i, g, half)], [("ug", i)], copy)
 
         def codes_u(i):
-            op((V,), 1100, [("ug", i)], [("uq", i)], lambda engine: quantize(
-                uq[i][:].rearrange("p g b -> p (g b)"), us[i][:].rearrange("p g b -> p (g b)"),
-                tiles["ug", i][:].rearrange("p g r t -> p (g r t)")), True)
-
-        def lay(i, g, t):
             def emit(engine):
-                if (i, g) not in wraw:
-                    load_w(i, g, w2)
-                wg = fresh(head, ("wg", i, g), [128, 4 * P], BF16, align_bytes=64)
+                quantized(
+                    u_q[i][:].rearrange("p g b -> p (g b)"), u_s[i][:].rearrange("p g b -> p (g b)"),
+                    tiles["ug", i][:].rearrange("p g b t -> p (g b t)"),
+                )
+            add({VECTOR: CODES}, [("ug", i)], [("u_q", i)], emit, port=True)
+
+        def lay_w(i, g, t):
+            def emit(engine):
+                wide = tile(("wide", "w", i, g), [128, 4 * P], BF16, 64)
                 moved(
                     engine,
-                    wg[:, 1024 * t : 1024 * (t + 1)].rearrange("p (i r j) -> p i j r", r=4, j=4),
-                    wraw[i, g][:].rearrange("p j (i t r) -> p t i j r", t=4, r=4)[:, t, :, :, :],
+                    wide[:, 1024 * t : 1024 * (t + 1)].rearrange("p (k r j) -> p k j r", r=4, j=4),
+                    raw["w", i, g][:].rearrange("p j (k t r) -> p t k j r", t=4, r=4)[:, t, :, :, :],
                 )
-            op((V, S), (640, 1300), [("wraw", i, g)], [("wg", i, g)], emit, True)
+            add(LAY, [("w", i, g)], [("wide", "w", i, g)], emit, port=True)
 
         def codes_w(i, g):
             def emit(engine):
-                quantize(wq[i][:, g, :], ws[i][:, g, :], tiles["wg", i, g][:])
+                quantized(w_q[i][:, g, :], w_s[i][:, g, :], tiles["wide", "w", i, g][:])
                 if (i, g) == (0, 0):
-                    load_w(1, 1, w2)
-            op((V,), 1100, [("wg", i, g)], [("wq", i, g)], emit, True)
+                    load_w(1, 1)
+            add({VECTOR: CODES}, [("wide", "w", i, g)], [("w_q", i)], emit, port=True)
 
-        def branch(i, g, b):
+        def branch(i, G, b):
+            batch = slice(128 * b, 128 * (b + 1))
+
             def emit(engine):
-                bank = fresh(ps, ("acc", "b", i, g, b), [128, 4, 128], F32, "acc")
-                r = slice(128 * b, 128 * (b + 1))
+                out = bank(("bank", "branch", i, G, b), [128, 4, 128])
                 for t in range(4):
-                    f = slice(256 * t + 128 * g, 256 * t + 128 * (g + 1))
-                    for k in range(2):
-                        nc.tensor.matmul_mx(
-                            out=bank[:, t, :],
-                            lhsT=wq[i][:, k, f].bitcast(FP8X4), lhsT_scale=ws[i][:, k, f],
-                            rhs=uq[i][:, k, r].bitcast(FP8X4), rhs_scale=us[i][:, k, r],
-                            start=(k == 0), stop=(k == 1),
-                        )
-            op((T,), 600, [("wq", i, 0), ("wq", i, 1), ("uq", i)], [("acc", "b", i, g, b)], emit)
+                    f = slice(256 * t + 128 * G, 256 * t + 128 * (G + 1))
+                    product(
+                        out[:, t, :],
+                        [w_q[i][:, g, f] for g in range(2)], [w_s[i][:, g, f] for g in range(2)],
+                        [u_q[i][:, g, batch] for g in range(2)], [u_s[i][:, g, batch] for g in range(2)],
+                    )
+            add({TENSOR: BRANCH}, [("w_q", i), ("u_q", i)], [("bank", "branch", i, G, b)], emit)
 
-        def coef(g, b):
-            def first(engine):
-                b1 = fresh(head, ("b1", g, b), [128, 128, 4], F32)
+        def coef(G, b):
+            def tanh(engine):
+                b1 = tile(("b1", G, b), [128, 128, 4], F32)
                 nc.scalar.activation(
-                    out=b1[:], in_=tiles["acc", "b", 0, g, b][:].rearrange("p t b -> p b t"), func=ACT.Tanh
+                    out=b1[:], in_=tiles["bank", "branch", 0, G, b][:].rearrange("p t b -> p b t"), func=ACT.Tanh
                 )
 
-            def product(engine):
-                cf = fresh(head, ("cf", g), [128, B, 4], BF16, align_bytes=64)
+            def times(engine):
+                cf = tile(("cf", G), [128, B, 4], BF16, 64)
                 nc.vector.tensor_tensor(
-                    cf[:, 128 * b : 128 * (b + 1), :], tiles["acc", "b", 1, g, b][:].rearrange("p t b -> p b t"),
-                    tiles["b1", g, b][:], ALU.mult,
+                    cf[:, 128 * b : 128 * (b + 1), :],
+                    tiles["bank", "branch", 1, G, b][:].rearrange("p t b -> p b t"), tiles["b1", G, b][:], ALU.mult,
                 )
 
-            branch(0, g, b)
-            op((S,), 540, [("acc", "b", 0, g, b)], [("b1", g, b)], first)
-            branch(1, g, b)
-            op((V,), 528, [("acc", "b", 1, g, b), ("b1", g, b)], [("cf", g)], product)
+            branch(0, G, b)
+            add({SCALAR: TANH_BRANCH}, [("bank", "branch", 0, G, b)], [("b1", G, b)], tanh)
+            branch(1, G, b)
+            add({VECTOR: COPY}, [("bank", "branch", 1, G, b), ("b1", G, b)], [("cf", G)], times)
 
-        def codes_coef(g):
-            op((V,), 560, [("cf", g)], [("cq", g)], lambda engine: quantize(
-                cq[:, g, :], cs[:, g, :], tiles["cf", g][:].rearrange("p b t -> p (b t)")), True)
-
-        def rows(h, bt):
-            bs = slice(128 * bt, 128 * (bt + 1))
-
-            def product(engine):
-                bank = fresh(ps, ("acc", "o", h, bt), [128, 512], F32, "acc")
-                for g in range(2):
-                    nc.tensor.matmul_mx(
-                        out=bank[:],
-                        lhsT=cq[:, g, bs].bitcast(FP8X4), lhsT_scale=cs[:, g, bs],
-                        rhs=tq[:, h, g, :].bitcast(FP8X4), rhs_scale=ts[:, h, g, :],
-                        start=(g == 0), stop=(g == 1),
-                    )
-
-            def copy(engine):
-                out = fresh(head, ("raw", h), [128, 4, 512], F32)
-                scaled(engine, out[:, bt, :], tiles["acc", "o", h, bt][:])
-                b0 = bt - bt % 2
-                copied[h, b0] = copied.get((h, b0), 0) + 1
-                if copied[h, b0] == 2:
-                    nc.sync.dma_start(
-                        out=out_0[128 * b0 : 128 * (b0 + 2), 512 * h : 512 * (h + 1)].rearrange(
-                            "(b p) n -> p b n", p=128
-                        ),
-                        in_=out[:, b0 : b0 + 2, :],
-                    )
-
-            op((T,), 534, [("cq", 0), ("cq", 1), ("tq", h)], [("acc", "o", h, bt)], product)
-            op((V, S), BANK, [("acc", "o", h, bt)], [("raw", h), ("pair", h, bt // 2)], copy)
-
-        def narrow(h, pair):
-            both = slice(2 * pair, 2 * pair + 2)
-
-            def copy(engine):
-                ob = fresh(head, ("ob", h), [128, 4, 512], BF16)
-                moved(engine, ob[:, both, :], tiles["raw", h][:, both, :])
-
-            def transposes(engine):
-                bank = fresh(ps, ("acc", "p", h, pair), [128, 2, 256], F32, "acc")
-                for r in range(2):
-                    words = tiles["ob", h][:, 2 * pair + r, :].bitcast(F32)
-                    for k in range(2):
-                        nc.tensor.transpose(bank[:, k, 128 * r : 128 * (r + 1)], words[:, k:256:2], id_f32[:])
-
-            def back(engine):
-                pl = fresh(head, ("wg", "p", h), [128, B, 4], BF16, "wg", align_bytes=64)
-                dst = pl[:, 256 * pair : 256 * (pair + 1), :].rearrange("p r t -> p (r t)").bitcast(F32)
-                moved(engine, dst.rearrange("p (r k) -> p r k", k=2),
-                      tiles["acc", "p", h, pair][:].rearrange("p k r -> p r k"))
-
-            op((V, S), (530, 1045), [("pair", h, pair)], [("ob", h), ("half", h, pair)], copy, True)
-            bank = ("acc", "p", h, pair, "turn")
-            op((T,), 504, [("half", h, pair)], [bank], transposes)
-            op((V, S), BANK, [bank], [("wg", "p", h)], back)
-
-        def store_planes(h):
+        def codes_coef(G):
             def emit(engine):
-                pq = fresh(head, ("pq", h), [128, B], U32, align_bytes=64)
-                pc = fresh(head, ("pc", h), [128, B], U8, "pc", align_bytes=64)
-                quantize(pq[:], pc[:], tiles["wg", "p", h][:].rearrange("p b t -> p (b t)"))
-                nc.sync.dma_start(out=out_1[h].rearrange("p m t -> p (m t)").bitcast(I32), in_=pq[:].bitcast(I32))
-                for q in range(4):
-                    nc.sync.dma_start(
-                        out=out_2[h, 4 * q : 4 * q + 4, :].bitcast(I32), in_=pc[32 * q : 32 * q + 4, :].bitcast(I32)
-                    )
-            op((V,), 560, [("wg", "p", h)], [("pq", h)], emit, True)
+                quantized(coef_q[:, G, :], coef_s[:, G, :], tiles["cf", G][:].rearrange("p b t -> p (b t)"))
+            add({VECTOR: CODES // 2}, [("cf", G)], [("coef_q",)], emit, port=True)
 
         def line(h, b):
             def emit(engine):
                 k = 4 * h + b
                 nc.vector.tensor_scalar(
-                    fresh(work, ("line", h, b), [128, 8, 128], F32)[:], rrow[:],
+                    tile(("line", h, b), [128, 8, 128], F32)[:], ratio_row[:],
                     xy[:, 1, k : k + 1], xy[:, 0, k : k + 1], ALU.mult, ALU.add,
                 )
-            op((V,), 530, [("rrow",), ("xy",)], [("line", h, b)], emit, True)
+            add({VECTOR: LINE}, [("ratio_row",), ("xy",)], [("line", h, b)], emit, port=True)
 
         def features(h, s):
-            g, t = divmod(s, 4)
+            g = s // 4
 
-            def transposes(engine):
+            def turn(engine):
                 for f in range(s, s + 2):
-                    pre = fresh(ps_x, ("pre", h, f), [128, 4, 128], F32)
                     for b in range(4):
-                        nc.tensor.transpose(pre[:, b, :], tiles["line", h, b][:, f, :], id_f32[:])
+                        nc.tensor.transpose(
+                            bank(("pre", h, f), [128, 4, 128])[:, b, :], tiles["line", h, b][:, f, :], id_f32[:]
+                        )
 
             def tanh(f):
                 def emit(engine):
-                    th = fresh(work, ("th", h, g), [128, 4, 512], F32)
                     nc.scalar.activation(
-                        out=th[:, f - 4 * g, :], in_=tiles["pre", h, f][:].rearrange("p b n -> p (b n)"),
-                        func=ACT.Tanh, scale=w0s[:, f : f + 1], bias=par[:, 2, f : f + 1],
+                        out=tile(("th", h, g), [128, 4, 512], F32)[:, f - 4 * g, :],
+                        in_=tiles["pre", h, f][:].rearrange("p b n -> p (b n)"), func=ACT.Tanh,
+                        scale=w0[:, f : f + 1], bias=par[:, 2, f : f + 1],
                     )
-                op((S,), 560, [("pre", h, f)], [("th", h, g)], emit)
+                add({SCALAR: TANH}, [("pre", h, f)], [("th", h, g)], emit)
 
-            op((T,), 616, [("line", h, b) for b in range(4)], [("pre", h, s), ("pre", h, s + 1)], transposes)
+            add({TENSOR: 8 * TURN}, [("line", h, b) for b in range(4)], [("pre", h, s), ("pre", h, s + 1)],
+                turn, turns=True)
             tanh(s)
             tanh(s + 1)
 
-        def gain_block(h, k):
+        def gains(h, k):
             g, b = divmod(k, 4)
-            cols = slice(128 * b, 128 * (b + 1))
+            some = slice(128 * b, 128 * (b + 1))
 
             def emit(engine):
-                grp = fresh(work, ("grp", h), [128, 2, 512, 4], BF16, align_bytes=64)
-                dst, src = grp[:, g, cols, :], tiles["th", h, g][:, :, cols]
-                if engine == G:
+                grp = tile(("grp", h), [128, 2, 512, 4], BF16, 64)
+                dst, src = grp[:, g, some, :], tiles["th", h, g][:, :, some]
+                if engine == GPSIMD:
                     nc.gpsimd.tensor_tensor(
                         dst, src.rearrange("p t n -> p n t"),
                         par[:, 3, 4 * g : 4 * g + 4].unsqueeze(1).to_broadcast([128, 128, 4]), ALU.mult,
@@ -434,34 +403,82 @@ def tile_multipleinputoperatorbranchtrunk_x1_kernel(
                 else:
                     nc.vector.tensor_tensor(
                         dst.rearrange("p (c i) t -> p c t i", i=4), src.rearrange("p t (c i) -> p c t i", i=4),
-                        prm[:, 4 * g : 4 * g + 4, 3].unsqueeze(1).unsqueeze(3).to_broadcast([128, 32, 4, 4]), ALU.mult,
+                        par_bank[:, 4 * g : 4 * g + 4, 3].unsqueeze(1).unsqueeze(3).to_broadcast([128, 32, 4, 4]),
+                        ALU.mult,
                     )
 
-            if k < GAIN_ON_GPSIMD:
-                op((G,), 1130, [("th", h, g)], [("grp", h)], emit, True)
-            elif k < GAIN_EITHER:
-                op((V, G), (540, 1130), [("th", h, g)], [("grp", h)], emit)
+            if k in GAIN_ON_GPSIMD:
+                add({GPSIMD: GAIN_GPSIMD}, [("th", h, g)], [("grp", h)], emit, port=True)
             else:
-                op((V,), 540, [("th", h, g)], [("grp", h)], emit)
+                add({VECTOR: GAIN}, [("th", h, g)], [("grp", h)], emit)
 
         def codes_trunk(h):
-            op((V,), 1100, [("grp", h)], [("tq", h)], lambda engine: quantize(
-                tq[:, h, :, :].rearrange("p g n -> p (g n)"), ts[:, h, :, :].rearrange("p g n -> p (g n)"),
-                tiles["grp", h][:].rearrange("p g n t -> p (g n t)")), True)
+            def emit(engine):
+                quantized(
+                    trunk_q[:, h, :, :].rearrange("p g n -> p (g n)"), trunk_s[:, h, :, :].rearrange("p g n -> p (g n)"),
+                    tiles["grp", h][:].rearrange("p g n t -> p (g n t)"),
+                )
+            add({VECTOR: CODES}, [("grp", h)], [("trunk_q", h)], emit, port=True)
 
-        def branches():
-            for i in range(2):
-                for g in range(2):
-                    for t in range(4):
-                        lay(i, g, t)
-                    codes_w(i, g)
-                    for half in range(2):
-                        turn_u(i, g, half)
-                codes_u(i)
-            for g in range(2):
-                for b in range(4):
-                    coef(g, b)
-                codes_coef(g)
+        def rows(h, bt):
+            batch = slice(128 * bt, 128 * (bt + 1))
+
+            def multiply(engine):
+                product(
+                    bank(("bank", "o", h, bt), [128, 512])[:],
+                    [coef_q[:, g, batch] for g in range(2)], [coef_s[:, g, batch] for g in range(2)],
+                    [trunk_q[:, h, g, :] for g in range(2)], [trunk_s[:, h, g, :] for g in range(2)],
+                )
+
+            def copy(engine):
+                out = tile(("raw", h), [128, 4, 512], F32)
+                if engine == VECTOR:
+                    nc.vector.tensor_scalar(out[:, bt, :], tiles["bank", "o", h, bt][:], 1.0 / 32.0, None, ALU.mult)
+                else:
+                    nc.scalar.mul(out[:, bt, :], tiles["bank", "o", h, bt][:], 1.0 / 32.0)
+                first = bt - bt % 2
+                stored[h, first] = stored.get((h, first), 0) + 1
+                if stored[h, first] == 2:
+                    nc.sync.dma_start(
+                        out=out_0[128 * first : 128 * (first + 2), 512 * h : 512 * (h + 1)].rearrange(
+                            "(b p) n -> p b n", p=128
+                        ),
+                        in_=out[:, first : first + 2, :],
+                    )
+
+            add({TENSOR: 2 * PASS}, [("coef_q",), ("trunk_q", h)], [("bank", "o", h, bt)], multiply)
+            add(both_copy, [("bank", "o", h, bt)], [("raw", h), ("rows", h, bt // 2)], copy)
+
+        def turn_rows(h, pair):
+            both = slice(2 * pair, 2 * pair + 2)
+
+            def narrow(engine):
+                moved(engine, tile(("ob", h), [128, 4, 512], BF16)[:, both, :], tiles["raw", h][:, both, :])
+
+            def turn(engine):
+                out = bank(("bank", "p", h, pair), [128, 2, 256])
+                word_turns(out, lambda r: tiles["ob", h][:, 2 * pair + r, :].bitcast(F32))
+
+            def copy(engine):
+                wide = tile(("wide", "p", h), [128, 4 * P], BF16, 64)
+                planes = wide[:, 0 : 4 * B].rearrange("p (b t) -> p b t", t=4)
+                words_back(engine, planes[:, 256 * pair : 256 * (pair + 1), :], tiles["bank", "p", h, pair][:])
+
+            add(NARROW, [("rows", h, pair)], [("ob", h), ("narrow", h, pair)], narrow, port=True)
+            add({TENSOR: 4 * TURN_STEPPED}, [("narrow", h, pair)], [("bank", "p", h, pair)], turn, turns=True)
+            add(both_copy, [("bank", "p", h, pair)], [("wide", "p", h)], copy)
+
+        def store_planes(h):
+            def emit(engine):
+                pq = tile(("pq", h), [128, B], U32, 64)
+                pc = tile(("pc", h), [128, B], U8, 64)
+                quantized(pq[:], pc[:], tiles["wide", "p", h][:, 0 : 4 * B])
+                nc.sync.dma_start(out=out_1[h].rearrange("p m t -> p (m t)").bitcast(I32), in_=pq[:].bitcast(I32))
+                for q in range(4):
+                    nc.sync.dma_start(
+                        out=out_2[h, 4 * q : 4 * q + 4, :].bitcast(I32), in_=pc[32 * q : 32 * q + 4, :].bitcast(I32)
+                    )
+            add({VECTOR: CODES // 2}, [("wide", "p", h)], [("pq", h), ("pc", h)], emit, port=True)
 
         def trunk(h):
             for b in range(4):
@@ -469,26 +486,39 @@ def tile_multipleinputoperatorbranchtrunk_x1_kernel(
             for s in range(0, 8, 2):
                 features(h, s)
             for k in range(8):
-                gain_block(h, k)
+                gains(h, k)
             codes_trunk(h)
 
+        def branches():
+            for i in range(2):
+                for g in range(2):
+                    for t in range(4):
+                        lay_w(i, g, t)
+                    codes_w(i, g)
+                    for half in range(2):
+                        turn_u(i, g, half)
+                codes_u(i)
+            for G in range(2):
+                for b in range(4):
+                    coef(G, b)
+                codes_coef(G)
+
         def results(h):
-            rows(h, 0)
-            rows(h, 1)
-            narrow(h, 0)
-            rows(h, 2)
-            rows(h, 3)
-            narrow(h, 1)
+            for pair in range(2):
+                rows(h, 2 * pair)
+                rows(h, 2 * pair + 1)
+                turn_rows(h, pair)
             store_planes(h)
 
+        parameters()
         trunk(0)
         branches()
-        trunk(1)
-        for h in range(2, 8):
+        for h in range(1, CHUNKS):
             trunk(h)
-            results(h - 2)
-        results(6)
-        results(7)
+            if h >= 2:
+                results(h - 2)
+        results(CHUNKS - 2)
+        results(CHUNKS - 1)
 
-        for k, engine in plan(ops, arrivals):
-            ops[k][5](engine)
+        for emit, engine in plan(work):
+            emit(engine)

from contextlib import ExitStack

import concourse.mybir as mybir
from concourse.masks import make_identity

B, M, P, N = 512, 1024, 1024, 4096
FLOPS = 2 * (2 * B * M * P) + 2 * B * N * P

F32 = mybir.dt.float32
BF16 = mybir.dt.bfloat16
U32 = mybir.dt.uint32
I32 = mybir.dt.int32
U8 = mybir.dt.uint8
FP8X4 = mybir.dt.float8_e4m3fn_x4
ALU = mybir.AluOpType
ACT = mybir.ActivationFunctionType

CHUNKS = N // 512
TINY = 2.0 ** -60

TENSOR, VECTOR, SCALAR, GPSIMD = "tensor", "vector", "scalar", "gpsimd"

GAIN_ON_GPSIMD = (0, 3, 6)

DEPTH = {
    "bank": 4,
    "pre": 3,
    "line": 8,
    "th": 3,
    "grp": 1,
    "wide": 2,
    "ug": 1,
    "raw": 5,
    "b1": 3, "cf": 1,
    "ob": 2,
    "pq": 3, "pc": 3,
}

COPY = 540
TANH, TANH_BRANCH = 580, 540
GAIN, GAIN_GPSIMD = 540, 1130
LINE = 530
NARROW = {VECTOR: 530, SCALAR: 1045}
LAY = {VECTOR: 600, SCALAR: 1250}
CODES = 1140
SORT, SAMPLES, DIVIDE = 300, 90, 1300
PASS, BRANCH = 267, 600
TURN = 77
TURN_STEPPED = 160
SWITCH = 96
HANDOVER = 170
OWN_RESULT = 180
SMALL_LOADED = 3300
FIRST_LOADED, NEXT_LOADED = 5000, 2150


def plan(work):
    writers, users, opened, room, needs = {}, {}, {}, {}, []
    for k, (engines, lengths, reads, writes, port, turns, emit) in enumerate(work):
        need = []
        for token in reads:
            need += writers.get(token, [])
        for token in writes:
            if token not in room:
                row = opened.setdefault(token[0], [])
                row.append(token)
                depth = DEPTH.get(token[0], 0)
                room[token] = list(users[row[-1 - depth]]) if depth and len(row) > depth else []
            need += room[token]
        for token in reads + writes:
            users.setdefault(token, []).append(k)
        for token in writes:
            writers.setdefault(token, []).append(k)
        needs.append(set(need))

    rank = [0] * len(work)
    for k in reversed(range(len(work))):
        rank[k] += min(work[k][1])
        for d in needs[k]:
            rank[d] = max(rank[d], rank[k] + HANDOVER)

    loads = [("w", 0, 0), ("u", 0), ("w", 0, 1), ("u", 1), ("w", 1, 0), ("w", 1, 1)]
    loaded = {token: FIRST_LOADED + NEXT_LOADED * k for k, token in enumerate(loads)}
    loaded[("small",)] = SMALL_LOADED
    free = {TENSOR: 0, VECTOR: 0, SCALAR: 0, GPSIMD: 0}
    finish, runs_on, order = {}, {}, []
    port_free, port_owner, turned = 0, None, None
    left = list(range(len(work)))
    while left:
        candidates = []
        for engine in free:
            options = []
            for k in left:
                engines, lengths, reads, writes, port, turns, emit = work[k]
                if engine not in engines or any(d not in finish for d in needs[k]):
                    continue
                asked = max([free[engine]] + [loaded.get(token, 0) for token in reads])
                for d in needs[k]:
                    if runs_on[d] != engine:
                        asked = max(asked, finish[d] + HANDOVER)
                    elif engine != TENSOR:
                        asked = max(asked, finish[d] + OWN_RESULT)
                held = port and engine in (VECTOR, GPSIMD) and port_owner != engine
                options.append((max(asked, port_free) if held else asked, -rank[k], asked, k))
            if options:
                start, urgency, asked, k = min(options)
                candidates.append((start, asked, engine, k))
        start, asked, engine, k = min(candidates)
        engines, lengths, reads, writes, port, turns, emit = work[k]
        finish[k] = start + lengths[engines.index(engine)]
        if engine == TENSOR and turns != turned:
            finish[k] += SWITCH
            turned = turns
        free[engine] = finish[k]
        runs_on[k] = engine
        if port and engine in (VECTOR, GPSIMD):
            port_free, port_owner = finish[k], engine
        left.remove(k)
        order.append((emit, engine))
    return order


def tile_multipleinputoperatorbranchtrunk_x1_kernel(
    tc, u1, u2, w1, w2, coords, wt, gain, out_0, out_1, out_2
):
    nc = tc.nc
    with ExitStack() as ctx:
        keep = ctx.enter_context(tc.tile_pool(name="keep", bufs=1))
        ring = ctx.enter_context(tc.tile_pool(name="ring", bufs=1))
        psum_keep = ctx.enter_context(tc.psum_pool(name="psum_keep", bufs=1))
        psum = ctx.enter_context(tc.psum_pool(name="psum", bufs=1))
        ctx.enter_context(tc.manual_schedule())

        small = keep.tile([128, P], BF16, name="small")
        nc.gpsimd.memset(small[:].bitcast(I32), 0)
        nc.scalar.dma_start(out=small[0:3, :], in_=wt)
        nc.scalar.dma_start(out=small[3:4, :], in_=gain.unsqueeze(0))
        nc.scalar.dma_start(out=small[32:64, 0:256], in_=coords.rearrange("(k p) c -> k (p c)", p=128))

        raw = {}

        def load_w(i, g):
            raw["w", i, g] = ring.tile([128, 4, P], BF16, name="w_raw", tag="raw", bufs=DEPTH["raw"])
            rows = (w1, w2)[i][512 * g : 512 * (g + 1), :]
            nc.sync.dma_start(out=raw["w", i, g][:], in_=rows.rearrange("(p j) c -> p j c", j=4))

        def load_u(i):
            raw["u", i] = ring.tile([128, 4, M], BF16, name="u_raw", tag="raw", bufs=DEPTH["raw"])
            nc.sync.dma_start(out=raw["u", i][:], in_=(u1, u2)[i].rearrange("(b p) m -> p b m", p=128))

        load_w(0, 0)
        load_u(0)
        load_w(0, 1)
        load_u(1)
        load_w(1, 0)

        id_bf16 = keep.tile([128, 128], BF16, name="id_bf16")
        make_identity(nc, id_bf16[:])
        id_f32 = keep.tile([128, 128], F32, name="id_f32")
        make_identity(nc, id_f32[:])

        trunk_q = keep.tile([128, CHUNKS, 2, 512], U32, name="trunk_q", align_bytes=64)
        trunk_s = keep.tile([128, CHUNKS, 2, 512], U8, name="trunk_s", align_bytes=64)
        coef_q = keep.tile([128, 2, B], U32, name="coef_q", align_bytes=64)
        coef_s = keep.tile([128, 2, B], U8, name="coef_s", align_bytes=64)
        u_q, u_s, w_q, w_s = {}, {}, {}, {}
        for i in range(2):
            u_q[i] = keep.tile([128, 2, B], U32, name=f"u_q{i}", align_bytes=64)
            u_s[i] = keep.tile([128, 2, B], U8, name=f"u_s{i}", align_bytes=64)
            w_q[i] = keep.tile([128, 2, P], U32, name=f"w_q{i}", align_bytes=64)
            w_s[i] = keep.tile([128, 2, P], U8, name=f"w_s{i}", align_bytes=64)
        sorted_rows = keep.tile([128, P], BF16, name="sorted_rows")
        xy = keep.tile([128, 2, 32], F32, name="xy")
        par = keep.tile([128, 4, 8], F32, name="par")
        w0 = keep.tile([128, 8], F32, name="w0")
        ratio = keep.tile([128, 8], F32, name="ratio")
        tmp_a = keep.tile([128, 8], F32, name="tmp_a")
        tmp_b = keep.tile([128, 8], F32, name="tmp_b")
        ratio_row = keep.tile([128, 8, 128], F32, name="ratio_row")
        par_bank = psum_keep.tile([128, 8, 128], BF16, name="par_bank")

        work, tiles, stored = [], {}, {}

        def add(lengths, reads, writes, emit, port=False, turns=False):
            work.append((tuple(lengths), tuple(lengths.values()), reads, writes, port, turns, emit))

        def tile(token, shape, dtype, align_bytes=0, pool=ring):
            if token not in tiles:
                more = {"align_bytes": align_bytes} if align_bytes else {}
                tiles[token] = pool.tile(
                    shape, dtype, name=token[0], tag=token[0], bufs=DEPTH[token[0]], **more
                )
            return tiles[token]

        def bank(token, shape, dtype=F32):
            return tile(token, shape, dtype, pool=psum)

        def moved(engine, dst, src):
            if engine == VECTOR:
                nc.vector.tensor_copy(out=dst, in_=src)
            else:
                nc.scalar.copy(out=dst, in_=src)

        def quantized(codes, scales, src):
            nc.vector.quantize_mx(out=codes.bitcast(FP8X4), scales=scales, in_=src)

        def product(out, left, left_s, right, right_s):
            for g in range(2):
                nc.tensor.matmul_mx(
                    out=out,
                    lhsT=left[g].bitcast(FP8X4), lhsT_scale=left_s[g],
                    rhs=right[g].bitcast(FP8X4), rhs_scale=right_s[g],
                    start=(g == 0), stop=(g == 1),
                )

        def word_turns(out, words):
            for r in range(2):
                for k in range(2):
                    nc.tensor.transpose(out[:, k, 128 * r : 128 * (r + 1)], words(r)[:, k:256:2], id_f32[:])

        def words_back(engine, dst, src):
            dst = dst.rearrange("p r t -> p (r t)").bitcast(F32)
            moved(engine, dst.rearrange("p (r k) -> p r k", k=2), src.rearrange("p k r -> p r k"))

        both_copy = {VECTOR: COPY, SCALAR: COPY}

        def sort_features(engine):
            nc.vector.tensor_copy(
                out=sorted_rows[:].rearrange("p (t i r) -> p t i r", t=4, r=4),
                in_=small[:].rearrange("p (i t r) -> p t i r", t=4, r=4),
            )

        def turn_samples(engine):
            for c in range(2):
                nc.tensor.transpose(
                    bank(("bank", "xy"), [128, 2, 128], BF16)[:, c, :], small[:, c:256:2], id_bf16[:]
                )

        def turn_parameters(engine):
            for s in range(8):
                g, t = divmod(s, 4)
                column = 256 * t + 128 * g
                nc.tensor.transpose(par_bank[:, s, :], sorted_rows[:, column : column + 128], id_bf16[:])

        def divide(engine):
            nc.vector.tensor_copy(out=par[:].rearrange("p v s -> p s v"), in_=par_bank[:, :, 0:4])
            nc.vector.tensor_single_scalar(tmp_a[:], par[:, 0, :], TINY, ALU.is_lt)
            nc.vector.scalar_tensor_tensor(
                out=tmp_b[:], in0=par[:, 0, :], scalar=-TINY, in1=tmp_a[:], op0=ALU.is_gt, op1=ALU.mult
            )
            nc.vector.scalar_tensor_tensor(
                out=w0[:], in0=tmp_b[:], scalar=2.0 * TINY, in1=par[:, 0, :], op0=ALU.mult, op1=ALU.add
            )
            nc.vector.reciprocal(tmp_a[:], w0[:])
            nc.vector.tensor_mul(ratio[:], tmp_a[:], par[:, 1, :])

        def parameters():
            add({VECTOR: SORT}, [("small",)], [("sorted",)], sort_features)
            add({TENSOR: 2 * TURN}, [("small",)], [("bank", "xy")], turn_samples, turns=True)
            add({SCALAR: SAMPLES}, [("bank", "xy")], [("xy",)],
                lambda engine: nc.scalar.copy(out=xy[:], in_=tiles["bank", "xy"][:, :, 32:64]))
            add({TENSOR: 8 * TURN}, [("sorted",)], [("par",)], turn_parameters, turns=True)
            add({VECTOR: DIVIDE}, [("par",)], [("ratio",)], divide)
            for g in range(2):
                ratio_row_half(g)

        def ratio_row_half(g):
            def turn(engine):
                for t in range(4):
                    nc.tensor.transpose(
                        bank(("bank", "r", g), [128, 4, 128])[:, t, :],
                        ratio[:, 4 * g + t : 4 * g + t + 1].to_broadcast([128, 128]), id_f32[:],
                    )

            def copy(engine):
                moved(engine, ratio_row[:, 4 * g : 4 * g + 4, :], tiles["bank", "r", g][:])

            add({TENSOR: 4 * TURN}, [("ratio",)], [("bank", "r", g)], turn, turns=True)
            add(both_copy, [("bank", "r", g)], [("ratio_row",)], copy)

        def turn_u(i, g, half):
            def turn(engine):
                out = bank(("bank", "u", i, g, half), [128, 2, 256])
                word_turns(
                    out, lambda r: raw["u", i][:, 2 * half + r, 512 * g : 512 * (g + 1)].bitcast(F32)
                )

            def copy(engine):
                ug = tile(("ug", i), [128, 2, B, 4], BF16, 64)
                words_back(engine, ug[:, g, 256 * half : 256 * (half + 1), :], tiles["bank", "u", i, g, half][:])

            add({TENSOR: 4 * TURN_STEPPED}, [("u", i)], [("bank", "u", i, g, half)], turn, turns=True)
            add(both_copy, [("bank", "u", i, g, half)], [("ug", i)], copy)

        def codes_u(i):
            def emit(engine):
                quantized(
                    u_q[i][:].rearrange("p g b -> p (g b)"), u_s[i][:].rearrange("p g b -> p (g b)"),
                    tiles["ug", i][:].rearrange("p g b t -> p (g b t)"),
                )
            add({VECTOR: CODES}, [("ug", i)], [("u_q", i)], emit, port=True)

        def lay_w(i, g, t):
            def emit(engine):
                wide = tile(("wide", "w", i, g), [128, 4 * P], BF16, 64)
                moved(
                    engine,
                    wide[:, 1024 * t : 1024 * (t + 1)].rearrange("p (k r j) -> p k j r", r=4, j=4),
                    raw["w", i, g][:].rearrange("p j (k t r) -> p t k j r", t=4, r=4)[:, t, :, :, :],
                )
            add(LAY, [("w", i, g)], [("wide", "w", i, g)], emit, port=True)

        def codes_w(i, g):
            def emit(engine):
                quantized(w_q[i][:, g, :], w_s[i][:, g, :], tiles["wide", "w", i, g][:])
                if (i, g) == (0, 0):
                    load_w(1, 1)
            add({VECTOR: CODES}, [("wide", "w", i, g)], [("w_q", i)], emit, port=True)

        def branch(i, G, b):
            batch = slice(128 * b, 128 * (b + 1))

            def emit(engine):
                out = bank(("bank", "branch", i, G, b), [128, 4, 128])
                for t in range(4):
                    f = slice(256 * t + 128 * G, 256 * t + 128 * (G + 1))
                    product(
                        out[:, t, :],
                        [w_q[i][:, g, f] for g in range(2)], [w_s[i][:, g, f] for g in range(2)],
                        [u_q[i][:, g, batch] for g in range(2)], [u_s[i][:, g, batch] for g in range(2)],
                    )
            add({TENSOR: BRANCH}, [("w_q", i), ("u_q", i)], [("bank", "branch", i, G, b)], emit)

        def coef(G, b):
            def tanh(engine):
                b1 = tile(("b1", G, b), [128, 128, 4], F32)
                nc.scalar.activation(
                    out=b1[:], in_=tiles["bank", "branch", 0, G, b][:].rearrange("p t b -> p b t"), func=ACT.Tanh
                )

            def times(engine):
                cf = tile(("cf", G), [128, B, 4], BF16, 64)
                nc.vector.tensor_tensor(
                    cf[:, 128 * b : 128 * (b + 1), :],
                    tiles["bank", "branch", 1, G, b][:].rearrange("p t b -> p b t"), tiles["b1", G, b][:], ALU.mult,
                )

            branch(0, G, b)
            add({SCALAR: TANH_BRANCH}, [("bank", "branch", 0, G, b)], [("b1", G, b)], tanh)
            branch(1, G, b)
            add({VECTOR: COPY}, [("bank", "branch", 1, G, b), ("b1", G, b)], [("cf", G)], times)

        def codes_coef(G):
            def emit(engine):
                quantized(coef_q[:, G, :], coef_s[:, G, :], tiles["cf", G][:].rearrange("p b t -> p (b t)"))
            add({VECTOR: CODES // 2}, [("cf", G)], [("coef_q",)], emit, port=True)

        def line(h, b):
            def emit(engine):
                k = 4 * h + b
                nc.vector.tensor_scalar(
                    tile(("line", h, b), [128, 8, 128], F32)[:], ratio_row[:],
                    xy[:, 1, k : k + 1], xy[:, 0, k : k + 1], ALU.mult, ALU.add,
                )
            add({VECTOR: LINE}, [("ratio_row",), ("xy",)], [("line", h, b)], emit, port=True)

        def features(h, s):
            g = s // 4

            def turn(engine):
                for f in range(s, s + 2):
                    for b in range(4):
                        nc.tensor.transpose(
                            bank(("pre", h, f), [128, 4, 128])[:, b, :], tiles["line", h, b][:, f, :], id_f32[:]
                        )

            def tanh(f):
                def emit(engine):
                    nc.scalar.activation(
                        out=tile(("th", h, g), [128, 4, 512], F32)[:, f - 4 * g, :],
                        in_=tiles["pre", h, f][:].rearrange("p b n -> p (b n)"), func=ACT.Tanh,
                        scale=w0[:, f : f + 1], bias=par[:, 2, f : f + 1],
                    )
                add({SCALAR: TANH}, [("pre", h, f)], [("th", h, g)], emit)

            add({TENSOR: 8 * TURN}, [("line", h, b) for b in range(4)], [("pre", h, s), ("pre", h, s + 1)],
                turn, turns=True)
            tanh(s)
            tanh(s + 1)

        def gains(h, k):
            g, b = divmod(k, 4)
            some = slice(128 * b, 128 * (b + 1))

            def emit(engine):
                grp = tile(("grp", h), [128, 2, 512, 4], BF16, 64)
                dst, src = grp[:, g, some, :], tiles["th", h, g][:, :, some]
                if engine == GPSIMD:
                    nc.gpsimd.tensor_tensor(
                        dst, src.rearrange("p t n -> p n t"),
                        par[:, 3, 4 * g : 4 * g + 4].unsqueeze(1).to_broadcast([128, 128, 4]), ALU.mult,
                    )
                else:
                    nc.vector.tensor_tensor(
                        dst.rearrange("p (c i) t -> p c t i", i=4), src.rearrange("p t (c i) -> p c t i", i=4),
                        par_bank[:, 4 * g : 4 * g + 4, 3].unsqueeze(1).unsqueeze(3).to_broadcast([128, 32, 4, 4]),
                        ALU.mult,
                    )

            if k in GAIN_ON_GPSIMD:
                add({GPSIMD: GAIN_GPSIMD}, [("th", h, g)], [("grp", h)], emit, port=True)
            else:
                add({VECTOR: GAIN}, [("th", h, g)], [("grp", h)], emit)

        def codes_trunk(h):
            def emit(engine):
                quantized(
                    trunk_q[:, h, :, :].rearrange("p g n -> p (g n)"), trunk_s[:, h, :, :].rearrange("p g n -> p (g n)"),
                    tiles["grp", h][:].rearrange("p g n t -> p (g n t)"),
                )
            add({VECTOR: CODES}, [("grp", h)], [("trunk_q", h)], emit, port=True)

        def rows(h, bt):
            batch = slice(128 * bt, 128 * (bt + 1))

            def multiply(engine):
                product(
                    bank(("bank", "o", h, bt), [128, 512])[:],
                    [coef_q[:, g, batch] for g in range(2)], [coef_s[:, g, batch] for g in range(2)],
                    [trunk_q[:, h, g, :] for g in range(2)], [trunk_s[:, h, g, :] for g in range(2)],
                )

            def copy(engine):
                out = tile(("raw", h), [128, 4, 512], F32)
                if engine == VECTOR:
                    nc.vector.tensor_scalar(out[:, bt, :], tiles["bank", "o", h, bt][:], 1.0 / 32.0, None, ALU.mult)
                else:
                    nc.scalar.mul(out[:, bt, :], tiles["bank", "o", h, bt][:], 1.0 / 32.0)
                first = bt - bt % 2
                stored[h, first] = stored.get((h, first), 0) + 1
                if stored[h, first] == 2:
                    nc.sync.dma_start(
                        out=out_0[128 * first : 128 * (first + 2), 512 * h : 512 * (h + 1)].rearrange(
                            "(b p) n -> p b n", p=128
                        ),
                        in_=out[:, first : first + 2, :],
                    )

            add({TENSOR: 2 * PASS}, [("coef_q",), ("trunk_q", h)], [("bank", "o", h, bt)], multiply)
            add(both_copy, [("bank", "o", h, bt)], [("raw", h), ("rows", h, bt // 2)], copy)

        def turn_rows(h, pair):
            both = slice(2 * pair, 2 * pair + 2)

            def narrow(engine):
                moved(engine, tile(("ob", h), [128, 4, 512], BF16)[:, both, :], tiles["raw", h][:, both, :])

            def turn(engine):
                out = bank(("bank", "p", h, pair), [128, 2, 256])
                word_turns(out, lambda r: tiles["ob", h][:, 2 * pair + r, :].bitcast(F32))

            def copy(engine):
                wide = tile(("wide", "p", h), [128, 4 * P], BF16, 64)
                planes = wide[:, 0 : 4 * B].rearrange("p (b t) -> p b t", t=4)
                words_back(engine, planes[:, 256 * pair : 256 * (pair + 1), :], tiles["bank", "p", h, pair][:])

            add(NARROW, [("rows", h, pair)], [("ob", h), ("narrow", h, pair)], narrow, port=True)
            add({TENSOR: 4 * TURN_STEPPED}, [("narrow", h, pair)], [("bank", "p", h, pair)], turn, turns=True)
            add(both_copy, [("bank", "p", h, pair)], [("wide", "p", h)], copy)

        def store_planes(h):
            def emit(engine):
                pq = tile(("pq", h), [128, B], U32, 64)
                pc = tile(("pc", h), [128, B], U8, 64)
                quantized(pq[:], pc[:], tiles["wide", "p", h][:, 0 : 4 * B])
                nc.sync.dma_start(out=out_1[h].rearrange("p m t -> p (m t)").bitcast(I32), in_=pq[:].bitcast(I32))
                for q in range(4):
                    nc.sync.dma_start(
                        out=out_2[h, 4 * q : 4 * q + 4, :].bitcast(I32), in_=pc[32 * q : 32 * q + 4, :].bitcast(I32)
                    )
            add({VECTOR: CODES // 2}, [("wide", "p", h)], [("pq", h), ("pc", h)], emit, port=True)

        def trunk(h):
            for b in range(4):
                line(h, b)
            for s in range(0, 8, 2):
                features(h, s)
            for k in range(8):
                gains(h, k)
            codes_trunk(h)

        def branches():
            for i in range(2):
                for g in range(2):
                    for t in range(4):
                        lay_w(i, g, t)
                    codes_w(i, g)
                    for half in range(2):
                        turn_u(i, g, half)
                codes_u(i)
            for G in range(2):
                for b in range(4):
                    coef(G, b)
                codes_coef(G)

        def results(h):
            for pair in range(2):
                rows(h, 2 * pair)
                rows(h, 2 * pair + 1)
                turn_rows(h, pair)
            store_planes(h)

        parameters()
        trunk(0)
        branches()
        for h in range(1, CHUNKS):
            trunk(h)
            if h >= 2:
                results(h - 2)
        results(CHUNKS - 2)
        results(CHUNKS - 1)

        for emit, engine in plan(work):
            emit(engine)
